import numpy as np
import ml_dtypes


def mxq(x, axis, fmt="e4m3"):
    dtype, down = {"e4m3": (ml_dtypes.float8_e4m3fn, 7), "e5m2": (ml_dtypes.float8_e5m2, 14)}[fmt]
    v = np.moveaxis(np.asarray(x, np.float32).astype(ml_dtypes.bfloat16).astype(np.float64), axis, -1)
    blocks = v.reshape(v.shape[:-1] + (-1, 32))
    amax = np.abs(blocks).max(-1, keepdims=True)
    byte = np.maximum(np.where(amax > 0, np.frexp(amax)[1] - 1 + 127, 0) - down, 1)
    scale = np.exp2(byte - 127.0)
    codes = (blocks / scale).astype(np.float32).astype(dtype).astype(np.float64)
    return np.moveaxis((codes * scale).reshape(v.shape), -1, axis)


WIDE = False


def mx_kscale(k):
    if not WIDE:
        return np.ones(k)
    levels = np.array([10, -10, 5, -5, 0])
    if k % 512:
        return np.exp2(np.random.permutation(np.resize(levels, k // 32))).repeat(32)
    a = np.empty((k // 512, 16))
    for p in range(k // 512):
        a[p, :8] = np.random.permutation(np.resize(levels, 8))
        for g in range(8):
            far = levels[np.abs(levels - a[p, g]) >= 10]
            a[p, g + 8] = far[np.random.randint(len(far))]
    return np.exp2(a.ravel()).repeat(32)


def f64(x):
    return np.asarray(x).astype(np.float64)


def striped(idx):
    return np.tile(idx.reshape(-1, 16).T, (8, 1)).astype(np.uint16)


def unstriped(offs):
    return offs[:16].T.reshape(-1).astype(np.int64)


def striped8(idx):
    return np.concatenate([x.reshape(-1, 16).T for x in idx]).astype(np.uint16)


def runs(offs, k):
    lists = np.stack([offs[16 * r : 16 * r + 16].T.reshape(-1) for r in range(8)]).astype(np.int64)
    return lists[np.arange(k) % 512 // 64]


def pack_weight(w):
    k, n = w.shape
    w = f64(np.asarray(w, np.float32).astype(ml_dtypes.bfloat16)).reshape(k // 32, 32, n)
    amax = np.abs(w).max(1)
    byte = np.clip(np.where(amax > 0, np.frexp(amax)[1] - 1 + 127 - 7, 1), 1, 254)
    scaled = (w * np.exp2(127.0 - byte)[:, None, :]).reshape(k, n).astype(np.float32)
    words = np.ascontiguousarray(scaled.reshape(k // 512, 128, 4, n).transpose(0, 1, 3, 2)).astype(ml_dtypes.float8_e4m3fn).view(np.uint8)
    return words, np.ascontiguousarray(byte.astype(np.uint8).reshape(k // 512, 16, n))


def unpack_weight(words, scales):
    g, p, n, _ = words.shape
    vals = np.ascontiguousarray(words).view(ml_dtypes.float8_e4m3fn).astype(np.float64) * np.repeat(np.exp2(scales.astype(np.float64) - 127.0), 8, axis=1)[..., None]
    return vals.transpose(0, 1, 3, 2).reshape(g * 512, n)


E2M1 = np.array([0.0, 0.5, 1.0, 1.5, 2.0, 3.0, 4.0, 6.0, -0.0, -0.5, -1.0, -1.5, -2.0, -3.0, -4.0, -6.0])


def pack_fp4(w):
    k, n = w.shape
    w = f64(np.asarray(w, np.float32).astype(ml_dtypes.bfloat16)).reshape(k // 32, 32, n)
    amax = np.abs(w).max(1)
    mant, ex = np.frexp(amax / 6.0)
    byte = np.clip(np.where(amax > 0, np.where(mant > 0.5, ex, ex - 1) + 127, 1), 1, 254)
    scaled = (w * np.exp2(127.0 - byte)[:, None, :]).reshape(k, n).astype(np.float32)
    c = np.ascontiguousarray(scaled.reshape(k // 512, 128, 4, n).transpose(0, 1, 3, 2)).astype(ml_dtypes.float4_e2m1fn).view(np.uint8) & 0xF
    words = (c[..., 0::2] | (c[..., 1::2] << 4)).reshape(k // 512, 128, 2 * n)
    return np.ascontiguousarray(words), np.ascontiguousarray(byte.astype(np.uint8).reshape(k // 512, 16, n))


def unpack_fp4(words, scales):
    g, _, n = scales.shape
    words = np.ascontiguousarray(words).reshape(g, 128, n, 2)
    nib = np.empty((g, 128, n, 4), np.uint8)
    nib[..., 0::2] = words & 0xF
    nib[..., 1::2] = words >> 4
    vals = E2M1[nib] * np.repeat(np.exp2(scales.astype(np.float64) - 127.0), 8, axis=1)[..., None]
    return vals.transpose(0, 1, 3, 2).reshape(g * 512, n)


def planes(y):
    n, m = y.shape
    v = y.astype(np.float32).astype(ml_dtypes.bfloat16).astype(np.float64).reshape(n // 32, 32, m)
    top = np.abs(v).max(1)
    byte = np.clip(np.where(top > 0, np.frexp(top)[1] - 1 + 127 - 7, 1), 1, 254)
    codes = (v * np.exp2(127.0 - byte)[:, None, :]).reshape(n, m).astype(np.float32).astype(ml_dtypes.float8_e4m3fn).view(np.uint8)
    words = codes.reshape(n // 512, 128, 4, m).transpose(0, 1, 3, 2)
    return np.ascontiguousarray(words), np.ascontiguousarray(byte.astype(np.uint8).reshape(n // 512, 16, m))


K, T, S, H, G = 512, 1024, 512, 512, 2048


def setup_inputs():
    n = np.random.standard_normal
    s = mx_kscale(K)[:, None]
    packed_xT = pack_weight(n((K, T)) * s)
    packed_w1 = pack_fp4(n((K, H)) / np.sqrt(K) / s)
    packed_w2 = pack_fp4(n((K, H)) / np.sqrt(K) / s)
    packed_dT = pack_weight(n((K, G)) / s)
    return {
        "x_words": packed_xT[0],
        "x_scales": packed_xT[1],
        "w1_words": packed_w1[0],
        "w1_scales": packed_w1[1],
        "w2_words": packed_w2[0],
        "w2_scales": packed_w2[1],
        "gs": (np.random.uniform(0.5, 1.5, (K, 1)) * s).astype(np.float32),
        "d_words": packed_dT[0],
        "d_scales": packed_dT[1],
        "tau": np.random.uniform(0.3, 0.9, (H, 1)).astype(np.float32),
        "offs": striped(np.random.permutation(T)[:S]),
        "two": striped(np.random.permutation(T)[:S]),
        "n1": striped(np.random.permutation(S)),
        "n2": striped(np.random.permutation(S)),
        "n3": striped(np.random.permutation(S)),
        "k1": striped8(np.random.randint(0, G, (8, H))),
        "n4": striped8(np.stack([np.random.permutation(S) for _ in range(8)])),
        "n5": striped8(np.stack([np.random.permutation(S) for _ in range(8)])),
    }


def reference(x_words, x_scales, w1_words, w1_scales, w2_words, w2_scales, gs, d_words, d_scales, tau, offs, two, n1, n2, n3, k1, n4, n5):
    d_k1 = unpack_weight(d_words, d_scales)[np.arange(K)[:, None], runs(k1, K)]
    xq = unpack_weight(x_words, x_scales)[:, unstriped(offs)]
    y = unpack_fp4(w1_words, w1_scales).T @ xq
    x_two = unpack_weight(x_words, x_scales)[:, unstriped(two)]
    d = unpack_fp4(w2_words, w2_scales).T @ x_two
    z = f64(gs) * (np.maximum(np.minimum(y - (0.5 * y[:, unstriped(n1)]), d[:, unstriped(n2)]), d[:, unstriped(n3)]))
    h = 0.0625 * ((d_k1.T @ mxq(z, 0, "e4m3")))
    low = h.min(axis=1, keepdims=True)
    ea = np.exp(f64(tau) * (low - (h[np.arange(H)[:, None], runs(n4, H)])))
    out_0 = h - (2.0 * (ea * (h[np.arange(H)[:, None], runs(n5, H)])))
    return (out_0,) + planes(out_0)

@@ -1,0 +1,231 @@
+from contextlib import ExitStack
+
+import concourse.mybir as mybir
+
+F32 = mybir.dt.float32
+BF16 = mybir.dt.bfloat16
+I32 = mybir.dt.int32
+U32 = mybir.dt.uint32
+U16 = mybir.dt.uint16
+U8 = mybir.dt.uint8
+FP8X4 = mybir.dt.float8_e4m3fn_x4
+FP4X4 = mybir.dt.float4_e2m1fn_x4
+ALU = mybir.AluOpType
+ACT = mybir.ActivationFunctionType
+
+P = 128
+PACK = 4
+K, T, S, H, G = 512, 1024, 512, 512, 2048
+HALF = S // 2
+FLOPS = 3 * 2 * 512 * 512 * 512
+
+Z_CHUNKS = [(0, 256), (256, 512)]
+OUT_CHUNKS = [(0, 256), (256, 512)]
+N2_ON_VECTOR = [(0, 0)]
+
+
+def tile_picked_twqclampbebz_none_po_kernel(
+    tc, x_words, x_scales, w1_words, w1_scales, w2_words, w2_scales, gs, d_words, d_scales, tau,
+    offs, two, n1, n2, n3, k1, n4, n5, out_0, out_1, out_2,
+):
+    nc = tc.nc
+
+    with ExitStack() as ctx:
+        keep = ctx.enter_context(tc.tile_pool(name="keep", bufs=1))
+        psum = ctx.enter_context(tc.psum_pool(name="psum", bufs=1))
+
+        def sb(shape, dtype, name):
+            return keep.tile(shape, dtype, name=name, align_bytes=64)
+
+        def bank(b):
+            return psum.tile([P, 512], F32, name="bank%d" % b, tag="bank%d" % b)
+
+        def load_list(src, name):
+            tile = sb([P, S // 16], U16, name)
+            nc.sync.dma_start(tile[:], src)
+            return tile
+
+        def entries(lst, a, b):
+            return lst[:, a // 16 : b // 16]
+
+        def zeroed_plane(width, name):
+            tile = sb([P, width], U8, name)
+            nc.vector.memset(tile[:].bitcast(I32), 0)
+            return tile
+
+        def load_plane(tile, src, queue, quadrants):
+            for q in quadrants:
+                queue.dma_start(tile[32 * q : 32 * q + 4, :].bitcast(I32), src[0, 4 * q : 4 * q + 4, :].bitcast(I32))
+
+        w1s_raw = zeroed_plane(H, "w1s_raw")
+        xs_tab = zeroed_plane(T, "xs_tab")
+        w2s_raw = zeroed_plane(H, "w2s_raw")
+        ds_tab = zeroed_plane(G, "ds_tab")
+        ds_plane = zeroed_plane(H, "ds_plane")
+
+        offs_l = load_list(offs, "offs_l")
+        load_plane(w1s_raw, w1_scales, nc.sync, (0, 1))
+        xw_tab = sb([P, T], I32, "xw_tab")
+        nc.sync.dma_start(xw_tab[:], x_words[0].rearrange("p c r -> p (c r)").bitcast(I32))
+        load_plane(xs_tab, x_scales, nc.sync, range(4))
+        w1w_raw = sb([P, 2 * H], U8, "w1w_raw")
+        nc.sync.dma_start(w1w_raw[:].bitcast(I32), w1_words[0].bitcast(I32))
+        load_plane(w1s_raw, w1_scales, nc.sync, (2, 3))
+        two_l = load_list(two, "two_l")
+        w2w_raw = sb([P, 2 * H], U8, "w2w_raw")
+        nc.sync.dma_start(w2w_raw[:].bitcast(I32), w2_words[0].bitcast(I32))
+        n1_l = load_list(n1, "n1_l")
+        load_plane(w2s_raw, w2_scales, nc.gpsimd, range(4))
+        k1_l = load_list(k1, "k1_l")
+        ds_rows = d_scales[0].rearrange("(g e) c -> e g c", e=2)
+        for e in range(2):
+            nc.gpsimd.dma_start(ds_tab[e:P:16, :].bitcast(I32), ds_rows[e].bitcast(I32))
+        dw_tab = sb([P, G], I32, "dw_tab")
+        nc.sync.dma_start(dw_tab[:], d_words[0].rearrange("p c r -> p (c r)").bitcast(I32))
+        n3_l = load_list(n3, "n3_l")
+        n2_l = load_list(n2, "n2_l")
+        gs_t = sb([P, PACK], F32, "gs_t")
+        nc.gpsimd.dma_start(gs_t[:], gs.rearrange("(p t) o -> p (t o)", t=PACK))
+        tau_t = sb([P, PACK], F32, "tau_t")
+        nc.gpsimd.dma_start(tau_t[:], tau.rearrange("(p t) o -> p (t o)", t=PACK))
+        n4_l = load_list(n4, "n4_l")
+        n5_l = load_list(n5, "n5_l")
+
+        def deal(engine_copy, raw, dtype, name):
+            dealt = sb(list(raw.shape), raw.dtype, name)
+            src = raw[:] if raw.dtype == dtype else raw[:].bitcast(dtype)
+            dst = dealt[:] if raw.dtype == dtype else dealt[:].bitcast(dtype)
+            engine_copy(dst.rearrange("p (t m) -> p t m", t=PACK), src.rearrange("p (m t) -> p t m", t=PACK))
+            return dealt
+
+        def pick(lst, a, b, name):
+            words = sb([P, b - a], U32, name + "_w")
+            nc.vector.tensor_copy(words[:], xw_tab[:].bitcast(U32).indirect(entries(lst, a, b)))
+            plane = sb([P, b - a], U8, name + "_s")
+            nc.vector.tensor_copy(plane[:], xs_tab[:].indirect(entries(lst, a, b)))
+            return words, plane
+
+        def mx(out, ww, ws, wtype, t, words, plane):
+            wide = ww.shape[1] // PACK
+            nc.tensor.matmul_mx(
+                out=out,
+                lhsT=ww[:, wide * t : wide * (t + 1)].bitcast(wtype),
+                lhsT_scale=ws[:, P * t : P * (t + 1)],
+                rhs=words[:].bitcast(FP8X4),
+                rhs_scale=plane[:],
+                start=True,
+                stop=True,
+            )
+
+        w1w = deal(nc.scalar.copy, w1w_raw, U16, "w1w")
+        w1s = deal(nc.vector.tensor_copy, w1s_raw, U8, "w1s")
+        y = [sb([P, S], F32, "y%d" % t) for t in range(PACK)]
+        for c in range(2):
+            words, plane = pick(offs_l, HALF * c, HALF * (c + 1), "xq%d" % c)
+            for pair in range(2):
+                acc = bank(2 * c + pair)
+                for e in range(2):
+                    mx(acc[:, HALF * e : HALF * (e + 1)], w1w, w1s, FP4X4, 2 * pair + e, words, plane)
+                for e in range(2):
+                    nc.scalar.copy(y[2 * pair + e][:, HALF * c : HALF * (c + 1)], acc[:, HALF * e : HALF * (e + 1)])
+
+        w2w = deal(nc.scalar.copy, w2w_raw, U16, "w2w")
+        w2s = deal(nc.vector.tensor_copy, w2s_raw, U8, "w2s")
+        words, plane = pick(two_l, 0, S, "xtwo")
+        d_acc = [bank(4 + t) for t in range(PACK)]
+        for t in range(PACK):
+            mx(d_acc[t][:], w2w, w2s, FP4X4, t, words, plane)
+
+        ds_got = sb([P, H], U8, "ds_got")
+        nc.vector.tensor_copy(ds_got[:], ds_tab[:].indirect(k1_l[:]))
+        ds_dealt = deal(nc.vector.tensor_copy, ds_got, U8, "ds_dealt")
+        for r in range(4):
+            first = 16 * (r // 2) + r % 2
+            nc.sync.dma_start(ds_plane[r:P:32, :].bitcast(I32), ds_dealt[first:P:32, :].bitcast(I32))
+        dw_got = sb([P, H], U32, "dw_got")
+        nc.vector.tensor_copy(dw_got[:], dw_tab[:].bitcast(U32).indirect(k1_l[:]))
+        dw = deal(nc.vector.tensor_copy, dw_got, U32, "dw")
+        neg_tau = sb([P, PACK], F32, "neg_tau")
+        nc.vector.tensor_scalar(neg_tau[:], tau_t[:], -1.0, None, ALU.mult)
+
+        d = [sb([P, S], F32, "d%d" % t) for t in range(PACK)]
+        h = [sb([P, S], F32, "h%d" % t) for t in range(PACK)]
+        lows = sb([P, PACK, len(Z_CHUNKS)], F32, "lows")
+
+        def fetch(window, lst, a, b, name, on_vector=False):
+            got = sb([P, b - a], F32, name)
+            if on_vector:
+                nc.vector.tensor_copy(got[:], window[:].indirect(entries(lst, a, b)))
+            else:
+                nc.scalar.activation(got[:], window[:].indirect(entries(lst, a, b)), ACT.Copy)
+            return got
+
+        def interleave(copy, rows, name):
+            width = rows.shape[2]
+            mixed = sb([P, width * PACK], BF16, name)
+            copy(mixed[:].rearrange("p (c i t) -> p c t i", i=4, t=PACK), rows[:].rearrange("p t (c i) -> p c t i", i=4))
+            return mixed
+
+        for c, (a, b) in enumerate(Z_CHUNKS):
+            w = b - a
+            y1 = [fetch(y[t], n1_l, a, b, "y1_%d_%d" % (c, t)) for t in range(PACK)]
+            if c == 0:
+                for t in range(PACK):
+                    nc.scalar.copy(d[t][:], d_acc[t][:])
+            u = []
+            for t in range(PACK):
+                u.append(sb([P, w], F32, "u_%d_%d" % (c, t)))
+                nc.vector.scalar_tensor_tensor(u[t][:], y1[t][:], -0.5, y[t][:, a:b], ALU.mult, ALU.add)
+            z_rows = sb([P, PACK, w], BF16, "z_rows%d" % c)
+            for t in range(PACK):
+                d2 = fetch(d[t], n2_l, a, b, "d2_%d_%d" % (c, t), (c, t) in N2_ON_VECTOR)
+                d3 = fetch(d[t], n3_l, a, b, "d3_%d_%d" % (c, t))
+                lo = sb([P, w], F32, "lo_%d_%d" % (c, t))
+                nc.vector.tensor_tensor(lo[:], u[t][:], d2[:], ALU.min)
+                hi = sb([P, w], F32, "hi_%d_%d" % (c, t))
+                nc.vector.tensor_tensor(hi[:], lo[:], d3[:], ALU.max)
+                nc.vector.tensor_scalar(z_rows[:, t, :], hi[:], gs_t[:, t : t + 1], None, ALU.mult)
+            z_mixed = interleave(nc.vector.tensor_copy, z_rows, "z_mixed%d" % c)
+            z_words = sb([P, w], U32, "z_words%d" % c)
+            z_plane = sb([P, w], U8, "z_plane%d" % c)
+            nc.vector.quantize_mx(out=z_words[:].bitcast(FP8X4), scales=z_plane[:], in_=z_mixed[:])
+            per_bank = 512 // w
+            for t0 in range(0, PACK, per_bank):
+                acc = bank((a * PACK + t0 * w) // 512)
+                for e in range(per_bank):
+                    mx(acc[:, w * e : w * (e + 1)], dw, ds_plane, FP8X4, t0 + e, z_words, z_plane)
+                for e in range(per_bank):
+                    t = t0 + e
+                    nc.vector.tensor_scalar(
+                        h[t][:, a:b], acc[:, w * e : w * (e + 1)], 0.0625, None, ALU.mult, ALU.min,
+                        accum_out=lows[:, t, c : c + 1],
+                    )
+
+        bias = sb([P, PACK], F32, "bias")
+        for t in range(PACK):
+            nc.vector.tensor_scalar(bias[:, t : t + 1], lows[:, t, 0:1], lows[:, t, 1:2], tau_t[:, t : t + 1], ALU.min, ALU.mult)
+
+        out_rows = out_0.rearrange("(p t) j -> p t j", t=PACK)
+        out_words = out_1[0].rearrange("p c r -> p (c r)").bitcast(I32)
+        o_plane = sb([P, S], U8, "o_plane")
+        for c, (a, b) in enumerate(OUT_CHUNKS):
+            w = b - a
+            o_rows = sb([P, PACK, w], F32, "o_rows%d" % c)
+            for t in range(PACK):
+                ea = sb([P, w], F32, "ea_%d_%d" % (c, t))
+                nc.scalar.activation(
+                    ea[:], h[t][:].indirect(entries(n4_l, a, b)), ACT.Exp,
+                    bias=bias[:, t : t + 1], scale=neg_tau[:, t : t + 1],
+                )
+                prod = sb([P, w], F32, "prod_%d_%d" % (c, t))
+                nc.vector.tensor_tensor(prod[:], h[t][:].indirect(entries(n5_l, a, b)), ea[:], ALU.mult)
+                nc.vector.scalar_tensor_tensor(o_rows[:, t, :], prod[:], -2.0, h[t][:, a:b], ALU.mult, ALU.add)
+            nc.sync.dma_start(out_rows[:, :, a:b], o_rows[:])
+            last = c == len(OUT_CHUNKS) - 1
+            o_mixed = interleave(nc.vector.tensor_copy if last else nc.scalar.copy, o_rows, "o_mixed%d" % c)
+            o_words = sb([P, w], I32, "o_words%d" % c)
+            nc.vector.quantize_mx(out=o_words[:].bitcast(FP8X4), scales=o_plane[:, a:b], in_=o_mixed[:])
+            nc.sync.dma_start(out_words[:, a:b], o_words[:])
+        for q in range(4):
+            queue = nc.scalar if q % 2 else nc.sync
+            queue.dma_start(out_2[0, 4 * q : 4 * q + 4, :].bitcast(I32), o_plane[32 * q : 32 * q + 4, :].bitcast(I32))

@@ -19,9 +19,20 @@ K, T, S, H, G = 512, 1024, 512, 512, 2048
 HALF = S // 2
 FLOPS = 3 * 2 * 512 * 512 * 512
 
-Z_CHUNKS = [(0, 256), (256, 512)]
+Z_CHUNKS = [(0, 256), (256, 384), (384, 512)]
 OUT_CHUNKS = [(0, 256), (256, 512)]
-N2_ON_VECTOR = [(0, 0)]
+N2_ON_VECTOR = [(0, 1), (0, 3)]
+D_OUT_ON_VECTOR = [1, 3]
+N5_ON_SCALAR = [(1, 3)]
+N5_EARLY = []
+LAST_MIX_SPLIT = 160
+RING = 4
+W1S_PIECES = 2
+GROUP = [1, 2, 2]
+U_ON_GPSIMD = False
+GS_ON_SCALAR = []
+H_OUT_ON_SCALAR = []
+Z_MIX_ON_SCALAR = [1]
 
 
 def tile_picked_twqclampbebz_none_po_kernel(
@@ -34,8 +45,8 @@ def tile_picked_twqclampbebz_none_po_kernel(
         keep = ctx.enter_context(tc.tile_pool(name="keep", bufs=1))
         psum = ctx.enter_context(tc.psum_pool(name="psum", bufs=1))
 
-        def sb(shape, dtype, name):
-            return keep.tile(shape, dtype, name=name, align_bytes=64)
+        def sb(shape, dtype, name, tag=None):
+            return keep.tile(shape, dtype, name=name, tag=tag or name, align_bytes=64)
 
         def bank(b):
             return psum.tile([P, 512], F32, name="bank%d" % b, tag="bank%d" % b)
@@ -57,53 +68,62 @@ def tile_picked_twqclampbebz_none_po_kernel(
             for q in quadrants:
                 queue.dma_start(tile[32 * q : 32 * q + 4, :].bitcast(I32), src[0, 4 * q : 4 * q + 4, :].bitcast(I32))
 
-        w1s_raw = zeroed_plane(H, "w1s_raw")
         xs_tab = zeroed_plane(T, "xs_tab")
+        w1s_raw = zeroed_plane(H, "w1s_raw")
         w2s_raw = zeroed_plane(H, "w2s_raw")
         ds_tab = zeroed_plane(G, "ds_tab")
         ds_plane = zeroed_plane(H, "ds_plane")
 
+        load_plane(xs_tab, x_scales, nc.scalar, (0, 1))
+        load_plane(xs_tab, x_scales, nc.sync, (2, 3))
         offs_l = load_list(offs, "offs_l")
-        load_plane(w1s_raw, w1_scales, nc.sync, (0, 1))
+        w1w_raw = sb([P, 2 * H], U8, "w1w_raw")
+        nc.scalar.dma_start(w1w_raw[:].bitcast(I32), w1_words[0].bitcast(I32))
+        load_plane(w1s_raw, w1_scales, nc.scalar, (0,))
         xw_tab = sb([P, T], I32, "xw_tab")
         nc.sync.dma_start(xw_tab[:], x_words[0].rearrange("p c r -> p (c r)").bitcast(I32))
-        load_plane(xs_tab, x_scales, nc.sync, range(4))
-        w1w_raw = sb([P, 2 * H], U8, "w1w_raw")
-        nc.sync.dma_start(w1w_raw[:].bitcast(I32), w1_words[0].bitcast(I32))
-        load_plane(w1s_raw, w1_scales, nc.sync, (2, 3))
+        load_plane(w1s_raw, w1_scales, nc.sync, (1, 2, 3))
         two_l = load_list(two, "two_l")
-        w2w_raw = sb([P, 2 * H], U8, "w2w_raw")
-        nc.sync.dma_start(w2w_raw[:].bitcast(I32), w2_words[0].bitcast(I32))
         n1_l = load_list(n1, "n1_l")
-        load_plane(w2s_raw, w2_scales, nc.gpsimd, range(4))
         k1_l = load_list(k1, "k1_l")
         ds_rows = d_scales[0].rearrange("(g e) c -> e g c", e=2)
         for e in range(2):
-            nc.gpsimd.dma_start(ds_tab[e:P:16, :].bitcast(I32), ds_rows[e].bitcast(I32))
+            nc.sync.dma_start(ds_tab[e:P:16, :].bitcast(I32), ds_rows[e].bitcast(I32))
+        w2w_raw = sb([P, 2 * H], U8, "w2w_raw")
+        nc.sync.dma_start(w2w_raw[:].bitcast(I32), w2_words[0].bitcast(I32))
         dw_tab = sb([P, G], I32, "dw_tab")
         nc.sync.dma_start(dw_tab[:], d_words[0].rearrange("p c r -> p (c r)").bitcast(I32))
-        n3_l = load_list(n3, "n3_l")
+        load_plane(w2s_raw, w2_scales, nc.sync, range(4))
         n2_l = load_list(n2, "n2_l")
+        n3_l = load_list(n3, "n3_l")
         gs_t = sb([P, PACK], F32, "gs_t")
-        nc.gpsimd.dma_start(gs_t[:], gs.rearrange("(p t) o -> p (t o)", t=PACK))
+        nc.sync.dma_start(gs_t[:], gs.rearrange("(p t) o -> p (t o)", t=PACK))
         tau_t = sb([P, PACK], F32, "tau_t")
-        nc.gpsimd.dma_start(tau_t[:], tau.rearrange("(p t) o -> p (t o)", t=PACK))
+        nc.sync.dma_start(tau_t[:], tau.rearrange("(p t) o -> p (t o)", t=PACK))
         n4_l = load_list(n4, "n4_l")
         n5_l = load_list(n5, "n5_l")
 
-        def deal(engine_copy, raw, dtype, name):
+        def deal(engine_copy, raw, dtype, name, pieces=1):
             dealt = sb(list(raw.shape), raw.dtype, name)
             src = raw[:] if raw.dtype == dtype else raw[:].bitcast(dtype)
             dst = dealt[:] if raw.dtype == dtype else dealt[:].bitcast(dtype)
-            engine_copy(dst.rearrange("p (t m) -> p t m", t=PACK), src.rearrange("p (m t) -> p t m", t=PACK))
+            e = src.shape[1] // H
+            dst = dst.rearrange("p (t m e) -> p t m e", t=PACK, e=e)
+            src = src.rearrange("p (m t e) -> p t m e", t=PACK, e=e)
+            n = PACK // pieces
+            for i in range(pieces):
+                engine_copy(dst[:, n * i : n * (i + 1)], src[:, n * i : n * (i + 1)])
             return dealt
 
-        def pick(lst, a, b, name):
-            words = sb([P, b - a], U32, name + "_w")
+        def pick_words(lst, a, b, name):
+            words = sb([P, b - a], U32, name)
             nc.vector.tensor_copy(words[:], xw_tab[:].bitcast(U32).indirect(entries(lst, a, b)))
-            plane = sb([P, b - a], U8, name + "_s")
+            return words
+
+        def pick_plane(lst, a, b, name):
+            plane = sb([P, b - a], U8, name)
             nc.vector.tensor_copy(plane[:], xs_tab[:].indirect(entries(lst, a, b)))
-            return words, plane
+            return plane
 
         def mx(out, ww, ws, wtype, t, words, plane):
             wide = ww.shape[1] // PACK
@@ -112,29 +132,29 @@ def tile_picked_twqclampbebz_none_po_kernel(
                 lhsT=ww[:, wide * t : wide * (t + 1)].bitcast(wtype),
                 lhsT_scale=ws[:, P * t : P * (t + 1)],
                 rhs=words[:].bitcast(FP8X4),
-                rhs_scale=plane[:],
+                rhs_scale=plane,
                 start=True,
                 stop=True,
             )
 
         w1w = deal(nc.scalar.copy, w1w_raw, U16, "w1w")
-        w1s = deal(nc.vector.tensor_copy, w1s_raw, U8, "w1s")
+        w1s = deal(nc.gpsimd.tensor_copy, w1s_raw, U8, "w1s", W1S_PIECES)
         y = [sb([P, S], F32, "y%d" % t) for t in range(PACK)]
+        xq_plane = pick_plane(offs_l, 0, S, "xq_plane")
         for c in range(2):
-            words, plane = pick(offs_l, HALF * c, HALF * (c + 1), "xq%d" % c)
-            for pair in range(2):
-                acc = bank(2 * c + pair)
-                for e in range(2):
-                    mx(acc[:, HALF * e : HALF * (e + 1)], w1w, w1s, FP4X4, 2 * pair + e, words, plane)
-                for e in range(2):
-                    nc.scalar.copy(y[2 * pair + e][:, HALF * c : HALF * (c + 1)], acc[:, HALF * e : HALF * (e + 1)])
+            words = pick_words(offs_l, HALF * c, HALF * (c + 1), "xq_words%d" % c)
+            for t in range(PACK):
+                acc = bank(PACK * c + t)
+                mx(acc[:, :HALF], w1w, w1s, FP4X4, t, words, xq_plane[:, HALF * c : HALF * (c + 1)])
+                nc.scalar.copy(y[t][:, HALF * c : HALF * (c + 1)], acc[:, :HALF])
 
-        w2w = deal(nc.scalar.copy, w2w_raw, U16, "w2w")
-        w2s = deal(nc.vector.tensor_copy, w2s_raw, U8, "w2s")
-        words, plane = pick(two_l, 0, S, "xtwo")
-        d_acc = [bank(4 + t) for t in range(PACK)]
+        w2w = deal(nc.gpsimd.tensor_copy, w2w_raw, U8, "w2w")
+        w2s = deal(nc.gpsimd.tensor_copy, w2s_raw, U8, "w2s")
+        words = pick_words(two_l, 0, S, "xtwo_words")
+        plane = pick_plane(two_l, 0, S, "xtwo_plane")
+        d_acc = [bank(t) for t in range(PACK)]
         for t in range(PACK):
-            mx(d_acc[t][:], w2w, w2s, FP4X4, t, words, plane)
+            mx(d_acc[t][:], w2w, w2s, FP4X4, t, words, plane[:])
 
         ds_got = sb([P, H], U8, "ds_got")
         nc.vector.tensor_copy(ds_got[:], ds_tab[:].indirect(k1_l[:]))
@@ -142,68 +162,110 @@ def tile_picked_twqclampbebz_none_po_kernel(
         for r in range(4):
             first = 16 * (r // 2) + r % 2
             nc.sync.dma_start(ds_plane[r:P:32, :].bitcast(I32), ds_dealt[first:P:32, :].bitcast(I32))
-        dw_got = sb([P, H], U32, "dw_got")
+        d = [sb([P, S], F32, "d%d" % t) for t in range(PACK)]
+        dw_got = sb([P, H], U32, "dw_got", "dw_got_then_u")
         nc.vector.tensor_copy(dw_got[:], dw_tab[:].bitcast(U32).indirect(k1_l[:]))
         dw = deal(nc.vector.tensor_copy, dw_got, U32, "dw")
         neg_tau = sb([P, PACK], F32, "neg_tau")
-        nc.vector.tensor_scalar(neg_tau[:], tau_t[:], -1.0, None, ALU.mult)
+        nc.gpsimd.tensor_scalar(neg_tau[:], tau_t[:], -1.0, 0.0, ALU.mult, ALU.add)
 
-        d = [sb([P, S], F32, "d%d" % t) for t in range(PACK)]
         h = [sb([P, S], F32, "h%d" % t) for t in range(PACK)]
         lows = sb([P, PACK, len(Z_CHUNKS)], F32, "lows")
+        bias = sb([P, PACK], F32, "bias")
 
-        def fetch(window, lst, a, b, name, on_vector=False):
-            got = sb([P, b - a], F32, name)
+        def fetch(got, window, lst, a, b, on_vector=False, scale=1.0):
             if on_vector:
-                nc.vector.tensor_copy(got[:], window[:].indirect(entries(lst, a, b)))
+                nc.vector.tensor_copy(got, window[:].indirect(entries(lst, a, b)))
             else:
-                nc.scalar.activation(got[:], window[:].indirect(entries(lst, a, b)), ACT.Copy)
-            return got
+                nc.scalar.activation(got, window[:].indirect(entries(lst, a, b)), ACT.Copy, scale=scale)
 
-        def interleave(copy, rows, name):
+        def interleave(rows, name, on_vector):
             width = rows.shape[2]
             mixed = sb([P, width * PACK], BF16, name)
-            copy(mixed[:].rearrange("p (c i t) -> p c t i", i=4, t=PACK), rows[:].rearrange("p t (c i) -> p c t i", i=4))
+            dst = mixed[:].rearrange("p (c i t) -> p c t i", i=4, t=PACK)
+            src = rows[:].rearrange("p t (c i) -> p c t i", i=4)
+            cut = on_vector // 4
+            if on_vector > 0:
+                nc.vector.tensor_copy(dst[:, :cut], src[:, :cut])
+            if on_vector < width:
+                nc.scalar.copy(dst[:, cut:], src[:, cut:])
             return mixed
 
-        for c, (a, b) in enumerate(Z_CHUNKS):
+        u = [sb([P, PACK, HALF], F32, "u0", "dw_got_then_u"), sb([P, PACK, HALF], F32, "u1")]
+
+        def make_u(c):
+            a, b = HALF * c, HALF * (c + 1)
+            for t in range(PACK):
+                y1 = sb([P, HALF], F32, "y1_%d_%d" % (c, t), "slot_a%d" % t if c else None)
+                if U_ON_GPSIMD:
+                    fetch(y1[:], y[t], n1_l, a, b, scale=-0.5)
+                    nc.gpsimd.tensor_tensor(u[c][:, t, :], y1[:], y[t][:, a:b], ALU.add)
+                else:
+                    fetch(y1[:], y[t], n1_l, a, b)
+                    nc.vector.scalar_tensor_tensor(u[c][:, t, :], y1[:], -0.5, y[t][:, a:b], ALU.mult, ALU.add)
+
+        def make_z(c):
+            a, b = Z_CHUNKS[c]
             w = b - a
-            y1 = [fetch(y[t], n1_l, a, b, "y1_%d_%d" % (c, t)) for t in range(PACK)]
-            if c == 0:
-                for t in range(PACK):
-                    nc.scalar.copy(d[t][:], d_acc[t][:])
-            u = []
-            for t in range(PACK):
-                u.append(sb([P, w], F32, "u_%d_%d" % (c, t)))
-                nc.vector.scalar_tensor_tensor(u[t][:], y1[t][:], -0.5, y[t][:, a:b], ALU.mult, ALU.add)
             z_rows = sb([P, PACK, w], BF16, "z_rows%d" % c)
-            for t in range(PACK):
-                d2 = fetch(d[t], n2_l, a, b, "d2_%d_%d" % (c, t), (c, t) in N2_ON_VECTOR)
-                d3 = fetch(d[t], n3_l, a, b, "d3_%d_%d" % (c, t))
-                lo = sb([P, w], F32, "lo_%d_%d" % (c, t))
-                nc.vector.tensor_tensor(lo[:], u[t][:], d2[:], ALU.min)
-                hi = sb([P, w], F32, "hi_%d_%d" % (c, t))
-                nc.vector.tensor_tensor(hi[:], lo[:], d3[:], ALU.max)
-                nc.vector.tensor_scalar(z_rows[:, t, :], hi[:], gs_t[:, t : t + 1], None, ALU.mult)
-            z_mixed = interleave(nc.vector.tensor_copy, z_rows, "z_mixed%d" % c)
+            lo, hi, d3 = {}, {}, {}
+            if c == 2:
+                late = sb([P, 2, PACK, w], F32, "late", "z_rows0")
+            for step in range(PACK + 2):
+                if step < PACK:
+                    t = step
+                    d2 = late[:, 0, t, :] if c == 2 else sb([P, w], F32, "d2_%d_%d" % (c, t), [None, "slot_b%d" % t][c])
+                    fetch(d2[:], d[t], n2_l, a, b, (c, t) in N2_ON_VECTOR)
+                    d3[t] = late[:, 1, t, :] if c == 2 else sb([P, w], F32, "d3_%d_%d" % (c, t), ["slot_a%d" % t, "slot_c%d" % t][c])
+                    fetch(d3[t][:], d[t], n3_l, a, b)
+                    lo[t] = sb([P, w], F32, "lo_%d_%d" % (c, t), None if c else "slot_b%d" % t)
+                    nc.vector.tensor_tensor(lo[t][:], u[a // HALF][:, t, a % HALF : a % HALF + w], d2[:], ALU.min)
+                if 1 <= step <= PACK:
+                    t = step - 1
+                    hi[t] = sb([P, w], F32, "hi_%d_%d" % (c, t), None if c else "slot_c%d" % t)
+                    nc.vector.tensor_tensor(hi[t][:], lo[t][:], d3[t][:], ALU.max)
+                if step >= 2:
+                    t = step - 2
+                    if c in GS_ON_SCALAR:
+                        nc.scalar.activation(z_rows[:, t, :], hi[t][:], ACT.Copy, scale=gs_t[:, t : t + 1])
+                    else:
+                        nc.vector.tensor_scalar(z_rows[:, t, :], hi[t][:], gs_t[:, t : t + 1], None, ALU.mult)
+            z_mixed = interleave(z_rows, "z_mixed%d" % c, 0 if c in Z_MIX_ON_SCALAR else w)
             z_words = sb([P, w], U32, "z_words%d" % c)
             z_plane = sb([P, w], U8, "z_plane%d" % c)
             nc.vector.quantize_mx(out=z_words[:].bitcast(FP8X4), scales=z_plane[:], in_=z_mixed[:])
-            per_bank = 512 // w
-            for t0 in range(0, PACK, per_bank):
-                acc = bank((a * PACK + t0 * w) // 512)
-                for e in range(per_bank):
-                    mx(acc[:, w * e : w * (e + 1)], dw, ds_plane, FP8X4, t0 + e, z_words, z_plane)
-                for e in range(per_bank):
-                    t = t0 + e
+            sums = []
+            for t in range(PACK):
+                acc = bank(PACK * ((c + 1) % 2) + t)
+                mx(acc[:, :w], dw, ds_plane, FP8X4, t, z_words, z_plane[:])
+                sums.append(acc[:, :w])
+            return sums
+
+        def make_h(c, sums):
+            a, b = Z_CHUNKS[c]
+            for t in range(PACK):
+                if c in H_OUT_ON_SCALAR:
+                    nc.scalar.activation(h[t][:, a:b], sums[t], ACT.Copy, scale=0.0625)
+                    if c + 1 not in H_OUT_ON_SCALAR:
+                        nc.vector.tensor_reduce(lows[:, t, c : c + 1], h[t][:, :b], mybir.AxisListType.X, ALU.min)
+                else:
                     nc.vector.tensor_scalar(
-                        h[t][:, a:b], acc[:, w * e : w * (e + 1)], 0.0625, None, ALU.mult, ALU.min,
+                        h[t][:, a:b], sums[t], 0.0625, lows[:, t, c - 1 : c] if c else None, ALU.mult, ALU.min,
                         accum_out=lows[:, t, c : c + 1],
                     )
+                if c == len(Z_CHUNKS) - 1:
+                    nc.scalar.activation(bias[:, t : t + 1], lows[:, t, c : c + 1], ACT.Copy, scale=tau_t[:, t : t + 1])
 
-        bias = sb([P, PACK], F32, "bias")
+        make_u(0)
         for t in range(PACK):
-            nc.vector.tensor_scalar(bias[:, t : t + 1], lows[:, t, 0:1], lows[:, t, 1:2], tau_t[:, t : t + 1], ALU.min, ALU.mult)
+            copy = nc.vector.tensor_copy if t in D_OUT_ON_VECTOR else nc.scalar.copy
+            copy(d[t][:], d_acc[t][:])
+        sums0 = make_z(0)
+        make_u(1)
+        make_h(0, sums0)
+        sums = [make_z(c) for c in range(1, len(Z_CHUNKS))]
+        for c in range(1, len(Z_CHUNKS)):
+            make_h(c, sums[c - 1])
 
         out_rows = out_0.rearrange("(p t) j -> p t j", t=PACK)
         out_words = out_1[0].rearrange("p c r -> p (c r)").bitcast(I32)
@@ -218,11 +280,16 @@ def tile_picked_twqclampbebz_none_po_kernel(
                     bias=bias[:, t : t + 1], scale=neg_tau[:, t : t + 1],
                 )
                 prod = sb([P, w], F32, "prod_%d_%d" % (c, t))
-                nc.vector.tensor_tensor(prod[:], h[t][:].indirect(entries(n5_l, a, b)), ea[:], ALU.mult)
+                if (c, t) in N5_ON_SCALAR + N5_EARLY:
+                    h5 = sb([P, w], F32, "h5_%d_%d" % (c, t))
+                    fetch(h5[:], h[t], n5_l, a, b, (c, t) in N5_EARLY)
+                    nc.vector.tensor_tensor(prod[:], h5[:], ea[:], ALU.mult)
+                else:
+                    nc.vector.tensor_tensor(prod[:], h[t][:].indirect(entries(n5_l, a, b)), ea[:], ALU.mult)
                 nc.vector.scalar_tensor_tensor(o_rows[:, t, :], prod[:], -2.0, h[t][:, a:b], ALU.mult, ALU.add)
-            nc.sync.dma_start(out_rows[:, :, a:b], o_rows[:])
-            last = c == len(OUT_CHUNKS) - 1
-            o_mixed = interleave(nc.vector.tensor_copy if last else nc.scalar.copy, o_rows, "o_mixed%d" % c)
+                if t % 2:
+                    nc.sync.dma_start(out_rows[:, t - 1 : t + 1, a:b], o_rows[:, t - 1 : t + 1, :])
+            o_mixed = interleave(o_rows, "o_mixed%d" % c, LAST_MIX_SPLIT if c == len(OUT_CHUNKS) - 1 else 0)
             o_words = sb([P, w], I32, "o_words%d" % c)
             nc.vector.quantize_mx(out=o_words[:].bitcast(FP8X4), scales=o_plane[:, a:b], in_=o_mixed[:])
             nc.sync.dma_start(out_words[:, a:b], o_words[:])

@@ -19,20 +19,21 @@ K, T, S, H, G = 512, 1024, 512, 512, 2048
 HALF = S // 2
 FLOPS = 3 * 2 * 512 * 512 * 512
 
-Z_CHUNKS = [(0, 256), (256, 384), (384, 512)]
+Z_CHUNKS = [(0, 256), (256, 512)]
 OUT_CHUNKS = [(0, 256), (256, 512)]
-N2_ON_VECTOR = [(0, 1), (0, 3)]
-D_OUT_ON_VECTOR = [1, 3]
+N2_ON_VECTOR = [(0, 0)]
+D_OUT_ON_VECTOR = [0, 1, 2, 3]
 N5_ON_SCALAR = [(1, 3)]
 N5_EARLY = []
 LAST_MIX_SPLIT = 160
-RING = 4
+SPARE = 16
+U_TAG = "dw_got"
 W1S_PIECES = 2
 GROUP = [1, 2, 2]
 U_ON_GPSIMD = False
 GS_ON_SCALAR = []
 H_OUT_ON_SCALAR = []
-Z_MIX_ON_SCALAR = [1]
+Z_MIX_ON_VECTOR = [256, 160]
 
 
 def tile_picked_twqclampbebz_none_po_kernel(
@@ -77,23 +78,23 @@ def tile_picked_twqclampbebz_none_po_kernel(
         load_plane(xs_tab, x_scales, nc.scalar, (0, 1))
         load_plane(xs_tab, x_scales, nc.sync, (2, 3))
         offs_l = load_list(offs, "offs_l")
-        w1w_raw = sb([P, 2 * H], U8, "w1w_raw")
-        nc.scalar.dma_start(w1w_raw[:].bitcast(I32), w1_words[0].bitcast(I32))
         load_plane(w1s_raw, w1_scales, nc.scalar, (0,))
         xw_tab = sb([P, T], I32, "xw_tab")
         nc.sync.dma_start(xw_tab[:], x_words[0].rearrange("p c r -> p (c r)").bitcast(I32))
+        w1w_raw = sb([P, 2 * H], U8, "w1w_raw")
+        nc.sync.dma_start(w1w_raw[:].bitcast(I32), w1_words[0].bitcast(I32))
         load_plane(w1s_raw, w1_scales, nc.sync, (1, 2, 3))
+        w2w_raw = sb([P, 2 * H], U8, "w2w_raw")
+        nc.sync.dma_start(w2w_raw[:].bitcast(I32), w2_words[0].bitcast(I32))
         two_l = load_list(two, "two_l")
-        n1_l = load_list(n1, "n1_l")
         k1_l = load_list(k1, "k1_l")
         ds_rows = d_scales[0].rearrange("(g e) c -> e g c", e=2)
         for e in range(2):
             nc.sync.dma_start(ds_tab[e:P:16, :].bitcast(I32), ds_rows[e].bitcast(I32))
-        w2w_raw = sb([P, 2 * H], U8, "w2w_raw")
-        nc.sync.dma_start(w2w_raw[:].bitcast(I32), w2_words[0].bitcast(I32))
+        load_plane(w2s_raw, w2_scales, nc.sync, range(4))
+        n1_l = load_list(n1, "n1_l")
         dw_tab = sb([P, G], I32, "dw_tab")
         nc.sync.dma_start(dw_tab[:], d_words[0].rearrange("p c r -> p (c r)").bitcast(I32))
-        load_plane(w2s_raw, w2_scales, nc.sync, range(4))
         n2_l = load_list(n2, "n2_l")
         n3_l = load_list(n3, "n3_l")
         gs_t = sb([P, PACK], F32, "gs_t")
@@ -131,7 +132,7 @@ def tile_picked_twqclampbebz_none_po_kernel(
                 out=out,
                 lhsT=ww[:, wide * t : wide * (t + 1)].bitcast(wtype),
                 lhsT_scale=ws[:, P * t : P * (t + 1)],
-                rhs=words[:].bitcast(FP8X4),
+                rhs=words.bitcast(FP8X4),
                 rhs_scale=plane,
                 start=True,
                 stop=True,
@@ -139,22 +140,23 @@ def tile_picked_twqclampbebz_none_po_kernel(
 
         w1w = deal(nc.scalar.copy, w1w_raw, U16, "w1w")
         w1s = deal(nc.gpsimd.tensor_copy, w1s_raw, U8, "w1s", W1S_PIECES)
-        y = [sb([P, S], F32, "y%d" % t) for t in range(PACK)]
-        xq_plane = pick_plane(offs_l, 0, S, "xq_plane")
-        for c in range(2):
-            words = pick_words(offs_l, HALF * c, HALF * (c + 1), "xq_words%d" % c)
-            for t in range(PACK):
-                acc = bank(PACK * c + t)
-                mx(acc[:, :HALF], w1w, w1s, FP4X4, t, words, xq_plane[:, HALF * c : HALF * (c + 1)])
-                nc.scalar.copy(y[t][:, HALF * c : HALF * (c + 1)], acc[:, :HALF])
+        y = [sb([P, S + SPARE], F32, "y%d" % t) for t in range(PACK)]
+        for t in range(PACK):
+            nc.gpsimd.memset(y[t][:, S:], 0.0)
+        plane = pick_plane(offs_l, 0, S, "xq_plane")
+        words = pick_words(offs_l, 0, S, "xq_words")
+        for t in range(PACK):
+            acc = bank(PACK + t)
+            mx(acc[:], w1w, w1s, FP4X4, t, words[:], plane[:])
+            nc.scalar.copy(y[t][:, :S], acc[:])
 
-        w2w = deal(nc.gpsimd.tensor_copy, w2w_raw, U8, "w2w")
+        w2w = deal(nc.scalar.copy, w2w_raw, U16, "w2w")
         w2s = deal(nc.gpsimd.tensor_copy, w2s_raw, U8, "w2s")
         words = pick_words(two_l, 0, S, "xtwo_words")
         plane = pick_plane(two_l, 0, S, "xtwo_plane")
         d_acc = [bank(t) for t in range(PACK)]
         for t in range(PACK):
-            mx(d_acc[t][:], w2w, w2s, FP4X4, t, words, plane[:])
+            mx(d_acc[t][:], w2w, w2s, FP4X4, t, words[:], plane[:])
 
         ds_got = sb([P, H], U8, "ds_got")
         nc.vector.tensor_copy(ds_got[:], ds_tab[:].indirect(k1_l[:]))
@@ -163,7 +165,10 @@ def tile_picked_twqclampbebz_none_po_kernel(
             first = 16 * (r // 2) + r % 2
             nc.sync.dma_start(ds_plane[r:P:32, :].bitcast(I32), ds_dealt[first:P:32, :].bitcast(I32))
         d = [sb([P, S], F32, "d%d" % t) for t in range(PACK)]
-        dw_got = sb([P, H], U32, "dw_got", "dw_got_then_u")
+        for t in range(PACK):
+            copy = nc.vector.tensor_copy if t in D_OUT_ON_VECTOR else nc.scalar.copy
+            copy(d[t][:], d_acc[t][:])
+        dw_got = sb([P, H], U32, "dw_got")
         nc.vector.tensor_copy(dw_got[:], dw_tab[:].bitcast(U32).indirect(k1_l[:]))
         dw = deal(nc.vector.tensor_copy, dw_got, U32, "dw")
         neg_tau = sb([P, PACK], F32, "neg_tau")
@@ -191,38 +196,34 @@ def tile_picked_twqclampbebz_none_po_kernel(
                 nc.scalar.copy(dst[:, cut:], src[:, cut:])
             return mixed
 
-        u = [sb([P, PACK, HALF], F32, "u0", "dw_got_then_u"), sb([P, PACK, HALF], F32, "u1")]
+        u = sb([P, PACK, S], F32, "u", U_TAG)
 
-        def make_u(c):
-            a, b = HALF * c, HALF * (c + 1)
-            for t in range(PACK):
-                y1 = sb([P, HALF], F32, "y1_%d_%d" % (c, t), "slot_a%d" % t if c else None)
-                if U_ON_GPSIMD:
-                    fetch(y1[:], y[t], n1_l, a, b, scale=-0.5)
-                    nc.gpsimd.tensor_tensor(u[c][:, t, :], y1[:], y[t][:, a:b], ALU.add)
-                else:
-                    fetch(y1[:], y[t], n1_l, a, b)
-                    nc.vector.scalar_tensor_tensor(u[c][:, t, :], y1[:], -0.5, y[t][:, a:b], ALU.mult, ALU.add)
+        def make_u(t):
+            y1 = sb([P, S], F32, "y1_%d" % t)
+            if U_ON_GPSIMD:
+                fetch(y1[:], y[t], n1_l, 0, S, scale=-0.5)
+                nc.gpsimd.tensor_tensor(u[:, t, :], y1[:], y[t][:, :S], ALU.add)
+            else:
+                fetch(y1[:], y[t], n1_l, 0, S)
+                nc.vector.scalar_tensor_tensor(u[:, t, :], y1[:], -0.5, y[t][:, :S], ALU.mult, ALU.add)
 
         def make_z(c):
             a, b = Z_CHUNKS[c]
             w = b - a
             z_rows = sb([P, PACK, w], BF16, "z_rows%d" % c)
             lo, hi, d3 = {}, {}, {}
-            if c == 2:
-                late = sb([P, 2, PACK, w], F32, "late", "z_rows0")
             for step in range(PACK + 2):
                 if step < PACK:
                     t = step
-                    d2 = late[:, 0, t, :] if c == 2 else sb([P, w], F32, "d2_%d_%d" % (c, t), [None, "slot_b%d" % t][c])
+                    d2 = sb([P, w], F32, "d2_%d_%d" % (c, t), "slot_a%d" % t if c else None)
                     fetch(d2[:], d[t], n2_l, a, b, (c, t) in N2_ON_VECTOR)
-                    d3[t] = late[:, 1, t, :] if c == 2 else sb([P, w], F32, "d3_%d_%d" % (c, t), ["slot_a%d" % t, "slot_c%d" % t][c])
+                    d3[t] = sb([P, w], F32, "d3_%d_%d" % (c, t), "slot_b%d" % t if c else None)
                     fetch(d3[t][:], d[t], n3_l, a, b)
-                    lo[t] = sb([P, w], F32, "lo_%d_%d" % (c, t), None if c else "slot_b%d" % t)
-                    nc.vector.tensor_tensor(lo[t][:], u[a // HALF][:, t, a % HALF : a % HALF + w], d2[:], ALU.min)
+                    lo[t] = sb([P, w], F32, "lo_%d_%d" % (c, t), None if c else "slot_a%d" % t)
+                    nc.vector.tensor_tensor(lo[t][:], u[:, t, a:b], d2[:], ALU.min)
                 if 1 <= step <= PACK:
                     t = step - 1
-                    hi[t] = sb([P, w], F32, "hi_%d_%d" % (c, t), None if c else "slot_c%d" % t)
+                    hi[t] = sb([P, w], F32, "hi_%d_%d" % (c, t), None if c else "slot_b%d" % t)
                     nc.vector.tensor_tensor(hi[t][:], lo[t][:], d3[t][:], ALU.max)
                 if step >= 2:
                     t = step - 2
@@ -230,14 +231,16 @@ def tile_picked_twqclampbebz_none_po_kernel(
                         nc.scalar.activation(z_rows[:, t, :], hi[t][:], ACT.Copy, scale=gs_t[:, t : t + 1])
                     else:
                         nc.vector.tensor_scalar(z_rows[:, t, :], hi[t][:], gs_t[:, t : t + 1], None, ALU.mult)
-            z_mixed = interleave(z_rows, "z_mixed%d" % c, 0 if c in Z_MIX_ON_SCALAR else w)
+            z_mixed = interleave(z_rows, "z_mixed%d" % c, Z_MIX_ON_VECTOR[c])
             z_words = sb([P, w], U32, "z_words%d" % c)
             z_plane = sb([P, w], U8, "z_plane%d" % c)
             nc.vector.quantize_mx(out=z_words[:].bitcast(FP8X4), scales=z_plane[:], in_=z_mixed[:])
             sums = []
             for t in range(PACK):
                 acc = bank(PACK * ((c + 1) % 2) + t)
-                mx(acc[:, :w], dw, ds_plane, FP8X4, t, z_words, z_plane[:])
+                for n0 in range(0, w, HALF):
+                    n1_ = min(w, n0 + HALF)
+                    mx(acc[:, n0:n1_], dw, ds_plane, FP8X4, t, z_words[:, n0:n1_], z_plane[:, n0:n1_])
                 sums.append(acc[:, :w])
             return sums
 
@@ -256,16 +259,11 @@ def tile_picked_twqclampbebz_none_po_kernel(
                 if c == len(Z_CHUNKS) - 1:
                     nc.scalar.activation(bias[:, t : t + 1], lows[:, t, c : c + 1], ACT.Copy, scale=tau_t[:, t : t + 1])
 
-        make_u(0)
         for t in range(PACK):
-            copy = nc.vector.tensor_copy if t in D_OUT_ON_VECTOR else nc.scalar.copy
-            copy(d[t][:], d_acc[t][:])
-        sums0 = make_z(0)
-        make_u(1)
-        make_h(0, sums0)
-        sums = [make_z(c) for c in range(1, len(Z_CHUNKS))]
-        for c in range(1, len(Z_CHUNKS)):
-            make_h(c, sums[c - 1])
+            make_u(t)
+        sums = [make_z(c) for c in range(len(Z_CHUNKS))]
+        for c in range(len(Z_CHUNKS)):
+            make_h(c, sums[c])
 
         out_rows = out_0.rearrange("(p t) j -> p t j", t=PACK)
         out_words = out_1[0].rearrange("p c r -> p (c r)").bitcast(I32)

@@ -25,15 +25,15 @@ N2_ON_VECTOR = [(0, 0)]
 D_OUT_ON_VECTOR = [0, 1, 2, 3]
 N5_ON_SCALAR = [(1, 3)]
 N5_EARLY = []
-LAST_MIX_SPLIT = 160
+LAST_MIX_SPLIT = 192
 SPARE = 16
 U_TAG = "dw_got"
-W1S_PIECES = 2
+W1S_PIECES = 1
 GROUP = [1, 2, 2]
 U_ON_GPSIMD = False
 GS_ON_SCALAR = []
-H_OUT_ON_SCALAR = []
-Z_MIX_ON_VECTOR = [256, 160]
+H_OUT_ON_SCALAR = [0]
+Z_MIX_ON_VECTOR = [256, 192]
 
 
 def tile_picked_twqclampbebz_none_po_kernel(
@@ -60,20 +60,20 @@ def tile_picked_twqclampbebz_none_po_kernel(
         def entries(lst, a, b):
             return lst[:, a // 16 : b // 16]
 
-        def zeroed_plane(width, name):
+        def zeroed_plane(width, name, engine):
             tile = sb([P, width], U8, name)
-            nc.vector.memset(tile[:].bitcast(I32), 0)
+            engine.memset(tile[:].bitcast(I32), 0)
             return tile
 
         def load_plane(tile, src, queue, quadrants):
             for q in quadrants:
                 queue.dma_start(tile[32 * q : 32 * q + 4, :].bitcast(I32), src[0, 4 * q : 4 * q + 4, :].bitcast(I32))
 
-        xs_tab = zeroed_plane(T, "xs_tab")
-        w1s_raw = zeroed_plane(H, "w1s_raw")
-        w2s_raw = zeroed_plane(H, "w2s_raw")
-        ds_tab = zeroed_plane(G, "ds_tab")
-        ds_plane = zeroed_plane(H, "ds_plane")
+        xs_tab = zeroed_plane(T, "xs_tab", nc.gpsimd)
+        w1s_raw = zeroed_plane(H, "w1s_raw", nc.gpsimd)
+        w2s_raw = zeroed_plane(H, "w2s_raw", nc.vector)
+        ds_tab = zeroed_plane(G, "ds_tab", nc.vector)
+        ds_plane = zeroed_plane(H, "ds_plane", nc.vector)
 
         load_plane(xs_tab, x_scales, nc.scalar, (0, 1))
         load_plane(xs_tab, x_scales, nc.sync, (2, 3))
@@ -89,9 +89,9 @@ def tile_picked_twqclampbebz_none_po_kernel(
         two_l = load_list(two, "two_l")
         k1_l = load_list(k1, "k1_l")
         ds_rows = d_scales[0].rearrange("(g e) c -> e g c", e=2)
-        for e in range(2):
-            nc.sync.dma_start(ds_tab[e:P:16, :].bitcast(I32), ds_rows[e].bitcast(I32))
+        nc.sync.dma_start(ds_tab[0:P:16, :].bitcast(I32), ds_rows[0].bitcast(I32))
         load_plane(w2s_raw, w2_scales, nc.sync, range(4))
+        nc.sync.dma_start(ds_tab[1:P:16, :].bitcast(I32), ds_rows[1].bitcast(I32))
         n1_l = load_list(n1, "n1_l")
         dw_tab = sb([P, G], I32, "dw_tab")
         nc.sync.dma_start(dw_tab[:], d_words[0].rearrange("p c r -> p (c r)").bitcast(I32))
@@ -139,7 +139,7 @@ def tile_picked_twqclampbebz_none_po_kernel(
             )
 
         w1w = deal(nc.scalar.copy, w1w_raw, U16, "w1w")
-        w1s = deal(nc.gpsimd.tensor_copy, w1s_raw, U8, "w1s", W1S_PIECES)
+        w1s = deal(nc.vector.tensor_copy, w1s_raw, U8, "w1s", W1S_PIECES)
         y = [sb([P, S + SPARE], F32, "y%d" % t) for t in range(PACK)]
         for t in range(PACK):
             nc.gpsimd.memset(y[t][:, S:], 0.0)
@@ -151,7 +151,7 @@ def tile_picked_twqclampbebz_none_po_kernel(
             nc.scalar.copy(y[t][:, :S], acc[:])
 
         w2w = deal(nc.scalar.copy, w2w_raw, U16, "w2w")
-        w2s = deal(nc.gpsimd.tensor_copy, w2s_raw, U8, "w2s")
+        w2s = deal(nc.vector.tensor_copy, w2s_raw, U8, "w2s")
         words = pick_words(two_l, 0, S, "xtwo_words")
         plane = pick_plane(two_l, 0, S, "xtwo_plane")
         d_acc = [bank(t) for t in range(PACK)]
@@ -164,7 +164,7 @@ def tile_picked_twqclampbebz_none_po_kernel(
         for r in range(4):
             first = 16 * (r // 2) + r % 2
             nc.sync.dma_start(ds_plane[r:P:32, :].bitcast(I32), ds_dealt[first:P:32, :].bitcast(I32))
-        d = [sb([P, S], F32, "d%d" % t) for t in range(PACK)]
+        d = [sb([P, S], F32, "d%d" % t, ["ds_got", "ds_tab", None, None][t]) for t in range(PACK)]
         for t in range(PACK):
             copy = nc.vector.tensor_copy if t in D_OUT_ON_VECTOR else nc.scalar.copy
             copy(d[t][:], d_acc[t][:])
@@ -172,7 +172,7 @@ def tile_picked_twqclampbebz_none_po_kernel(
         nc.vector.tensor_copy(dw_got[:], dw_tab[:].bitcast(U32).indirect(k1_l[:]))
         dw = deal(nc.vector.tensor_copy, dw_got, U32, "dw")
         neg_tau = sb([P, PACK], F32, "neg_tau")
-        nc.gpsimd.tensor_scalar(neg_tau[:], tau_t[:], -1.0, 0.0, ALU.mult, ALU.add)
+        nc.vector.tensor_scalar(neg_tau[:], tau_t[:], -1.0, None, ALU.mult)
 
         h = [sb([P, S], F32, "h%d" % t) for t in range(PACK)]
         lows = sb([P, PACK, len(Z_CHUNKS)], F32, "lows")

@@ -15,25 +15,16 @@ ACT = mybir.ActivationFunctionType
 
 P = 128
 PACK = 4
-K, T, S, H, G = 512, 1024, 512, 512, 2048
+QUADS = 4
+T, S, H, G = 1024, 512, 512, 2048
 HALF = S // 2
 FLOPS = 3 * 2 * 512 * 512 * 512
 
-Z_CHUNKS = [(0, 256), (256, 512)]
-OUT_CHUNKS = [(0, 256), (256, 512)]
-N2_ON_VECTOR = [(0, 0)]
-D_OUT_ON_VECTOR = [0, 1, 2, 3]
-N5_ON_SCALAR = [(1, 3)]
-N5_EARLY = []
-LAST_MIX_SPLIT = 192
 SPARE = 16
-U_TAG = "dw_got"
-W1S_PIECES = 1
-GROUP = [1, 2, 2]
-U_ON_GPSIMD = False
-GS_ON_SCALAR = []
-H_OUT_ON_SCALAR = [0]
-Z_MIX_ON_VECTOR = [256, 192]
+U_TILES_ON_GPSIMD = 3
+N2_TILES_ON_VECTOR = 3
+Z_MIX_ON_VECTOR = (HALF, 160)
+OUT_MIX_ON_VECTOR = (0, 192)
 
 
 def tile_picked_twqclampbebz_none_po_kernel(
@@ -46,19 +37,32 @@ def tile_picked_twqclampbebz_none_po_kernel(
         keep = ctx.enter_context(tc.tile_pool(name="keep", bufs=1))
         psum = ctx.enter_context(tc.psum_pool(name="psum", bufs=1))
 
-        def sb(shape, dtype, name, tag=None):
-            return keep.tile(shape, dtype, name=name, tag=tag or name, align_bytes=64)
+        def sb(shape, dtype, name, after=None):
+            return keep.tile(shape, dtype, name=name, tag=after or name, align_bytes=64)
 
         def bank(b):
-            return psum.tile([P, 512], F32, name="bank%d" % b, tag="bank%d" % b)
+            return psum.tile([P, S], F32, name="bank%d" % b, tag="bank%d" % b)
+
+        def columns(half):
+            return slice(HALF * half, HALF * (half + 1))
+
+        def entries(lst, half):
+            return lst[:, HALF // 16 * half : HALF // 16 * (half + 1)]
 
         def load_list(src, name):
             tile = sb([P, S // 16], U16, name)
             nc.sync.dma_start(tile[:], src)
             return tile
 
-        def entries(lst, a, b):
-            return lst[:, a // 16 : b // 16]
+        def load_words(src, shape, dtype, name):
+            tile = sb(shape, dtype, name)
+            nc.sync.dma_start(tile[:].bitcast(I32), src.bitcast(I32))
+            return tile
+
+        def load_by_row_tile(src, name):
+            tile = sb([P, PACK], F32, name)
+            nc.sync.dma_start(tile[:], src.rearrange("(p t) o -> p (t o)", t=PACK))
+            return tile
 
         def zeroed_plane(width, name, engine):
             tile = sb([P, width], U8, name)
@@ -67,7 +71,9 @@ def tile_picked_twqclampbebz_none_po_kernel(
 
         def load_plane(tile, src, queue, quadrants):
             for q in quadrants:
-                queue.dma_start(tile[32 * q : 32 * q + 4, :].bitcast(I32), src[0, 4 * q : 4 * q + 4, :].bitcast(I32))
+                queue.dma_start(
+                    tile[32 * q : 32 * q + QUADS, :].bitcast(I32), src[0, QUADS * q : QUADS * (q + 1), :].bitcast(I32)
+                )
 
         xs_tab = zeroed_plane(T, "xs_tab", nc.gpsimd)
         w1s_raw = zeroed_plane(H, "w1s_raw", nc.gpsimd)
@@ -79,218 +85,179 @@ def tile_picked_twqclampbebz_none_po_kernel(
         load_plane(xs_tab, x_scales, nc.sync, (2, 3))
         offs_l = load_list(offs, "offs_l")
         load_plane(w1s_raw, w1_scales, nc.scalar, (0,))
-        xw_tab = sb([P, T], I32, "xw_tab")
-        nc.sync.dma_start(xw_tab[:], x_words[0].rearrange("p c r -> p (c r)").bitcast(I32))
-        w1w_raw = sb([P, 2 * H], U8, "w1w_raw")
-        nc.sync.dma_start(w1w_raw[:].bitcast(I32), w1_words[0].bitcast(I32))
+        xw_tab = load_words(x_words[0].rearrange("p c r -> p (c r)"), [P, T], U32, "xw_tab")
+        w1w_raw = load_words(w1_words[0], [P, H], U16, "w1w_raw")
         load_plane(w1s_raw, w1_scales, nc.sync, (1, 2, 3))
-        w2w_raw = sb([P, 2 * H], U8, "w2w_raw")
-        nc.sync.dma_start(w2w_raw[:].bitcast(I32), w2_words[0].bitcast(I32))
+        w2w_raw = load_words(w2_words[0], [P, H], U16, "w2w_raw")
         two_l = load_list(two, "two_l")
         k1_l = load_list(k1, "k1_l")
         ds_rows = d_scales[0].rearrange("(g e) c -> e g c", e=2)
-        nc.sync.dma_start(ds_tab[0:P:16, :].bitcast(I32), ds_rows[0].bitcast(I32))
-        load_plane(w2s_raw, w2_scales, nc.sync, range(4))
-        nc.sync.dma_start(ds_tab[1:P:16, :].bitcast(I32), ds_rows[1].bitcast(I32))
+        for e in range(2):
+            nc.sync.dma_start(ds_tab[e:P:16, :].bitcast(I32), ds_rows[e].bitcast(I32))
+        load_plane(w2s_raw, w2_scales, nc.sync, range(QUADS))
         n1_l = load_list(n1, "n1_l")
-        dw_tab = sb([P, G], I32, "dw_tab")
-        nc.sync.dma_start(dw_tab[:], d_words[0].rearrange("p c r -> p (c r)").bitcast(I32))
+        dw_tab = load_words(d_words[0].rearrange("p c r -> p (c r)"), [P, G], U32, "dw_tab")
         n2_l = load_list(n2, "n2_l")
         n3_l = load_list(n3, "n3_l")
-        gs_t = sb([P, PACK], F32, "gs_t")
-        nc.sync.dma_start(gs_t[:], gs.rearrange("(p t) o -> p (t o)", t=PACK))
-        tau_t = sb([P, PACK], F32, "tau_t")
-        nc.sync.dma_start(tau_t[:], tau.rearrange("(p t) o -> p (t o)", t=PACK))
+        gs_t = load_by_row_tile(gs, "gs_t")
+        tau_t = load_by_row_tile(tau, "tau_t")
         n4_l = load_list(n4, "n4_l")
         n5_l = load_list(n5, "n5_l")
 
-        def deal(engine_copy, raw, dtype, name, pieces=1):
-            dealt = sb(list(raw.shape), raw.dtype, name)
-            src = raw[:] if raw.dtype == dtype else raw[:].bitcast(dtype)
-            dst = dealt[:] if raw.dtype == dtype else dealt[:].bitcast(dtype)
-            e = src.shape[1] // H
-            dst = dst.rearrange("p (t m e) -> p t m e", t=PACK, e=e)
-            src = src.rearrange("p (m t e) -> p t m e", t=PACK, e=e)
+        def deal(copy, raw, name, pieces=1, after=None):
+            dealt = sb([P, H], raw.dtype, name, after)
+            dst = dealt[:].rearrange("p (t m) -> p t m", t=PACK)
+            src = raw[:].rearrange("p (m t) -> p t m", t=PACK)
             n = PACK // pieces
             for i in range(pieces):
-                engine_copy(dst[:, n * i : n * (i + 1)], src[:, n * i : n * (i + 1)])
+                copy(dst[:, n * i : n * (i + 1)], src[:, n * i : n * (i + 1)])
             return dealt
 
-        def pick_words(lst, a, b, name):
-            words = sb([P, b - a], U32, name)
-            nc.vector.tensor_copy(words[:], xw_tab[:].bitcast(U32).indirect(entries(lst, a, b)))
-            return words
+        def pick(table, lst, name):
+            picked = sb([P, S], table.dtype, name)
+            nc.vector.tensor_copy(picked[:], table[:].indirect(lst[:]))
+            return picked
 
-        def pick_plane(lst, a, b, name):
-            plane = sb([P, b - a], U8, name)
-            nc.vector.tensor_copy(plane[:], xs_tab[:].indirect(entries(lst, a, b)))
-            return plane
-
-        def mx(out, ww, ws, wtype, t, words, plane):
-            wide = ww.shape[1] // PACK
+        def product(acc, dealt_words, dealt_plane, fmt, t, words, plane):
+            rows = slice(P * t, P * (t + 1))
             nc.tensor.matmul_mx(
-                out=out,
-                lhsT=ww[:, wide * t : wide * (t + 1)].bitcast(wtype),
-                lhsT_scale=ws[:, P * t : P * (t + 1)],
-                rhs=words.bitcast(FP8X4),
-                rhs_scale=plane,
+                out=acc,
+                lhsT=dealt_words[:, rows].bitcast(fmt),
+                lhsT_scale=dealt_plane[:, rows],
+                rhs=words[:].bitcast(FP8X4),
+                rhs_scale=plane[:],
                 start=True,
                 stop=True,
             )
 
-        w1w = deal(nc.scalar.copy, w1w_raw, U16, "w1w")
-        w1s = deal(nc.vector.tensor_copy, w1s_raw, U8, "w1s", W1S_PIECES)
+        w1w = deal(nc.scalar.copy, w1w_raw, "w1w")
+        w1s = deal(nc.gpsimd.tensor_copy, w1s_raw, "w1s", pieces=2)
         y = [sb([P, S + SPARE], F32, "y%d" % t) for t in range(PACK)]
         for t in range(PACK):
             nc.gpsimd.memset(y[t][:, S:], 0.0)
-        plane = pick_plane(offs_l, 0, S, "xq_plane")
-        words = pick_words(offs_l, 0, S, "xq_words")
+        xq_plane = pick(xs_tab, offs_l, "xq_plane")
+        xq_words = pick(xw_tab, offs_l, "xq_words")
         for t in range(PACK):
             acc = bank(PACK + t)
-            mx(acc[:], w1w, w1s, FP4X4, t, words[:], plane[:])
+            product(acc[:], w1w, w1s, FP4X4, t, xq_words, xq_plane)
             nc.scalar.copy(y[t][:, :S], acc[:])
 
-        w2w = deal(nc.scalar.copy, w2w_raw, U16, "w2w")
-        w2s = deal(nc.vector.tensor_copy, w2s_raw, U8, "w2s")
-        words = pick_words(two_l, 0, S, "xtwo_words")
-        plane = pick_plane(two_l, 0, S, "xtwo_plane")
+        w2w = deal(nc.scalar.copy, w2w_raw, "w2w")
+        w2s = deal(nc.gpsimd.tensor_copy, w2s_raw, "w2s")
+        xtwo_words = pick(xw_tab, two_l, "xtwo_words")
+        xtwo_plane = pick(xs_tab, two_l, "xtwo_plane")
         d_acc = [bank(t) for t in range(PACK)]
         for t in range(PACK):
-            mx(d_acc[t][:], w2w, w2s, FP4X4, t, words[:], plane[:])
+            product(d_acc[t][:], w2w, w2s, FP4X4, t, xtwo_words, xtwo_plane)
 
-        ds_got = sb([P, H], U8, "ds_got")
-        nc.vector.tensor_copy(ds_got[:], ds_tab[:].indirect(k1_l[:]))
-        ds_dealt = deal(nc.vector.tensor_copy, ds_got, U8, "ds_dealt")
-        for r in range(4):
+        ds_dealt = deal(nc.vector.tensor_copy, pick(ds_tab, k1_l, "ds_got"), "ds_dealt")
+        for r in range(QUADS):
             first = 16 * (r // 2) + r % 2
             nc.sync.dma_start(ds_plane[r:P:32, :].bitcast(I32), ds_dealt[first:P:32, :].bitcast(I32))
-        d = [sb([P, S], F32, "d%d" % t, ["ds_got", "ds_tab", None, None][t]) for t in range(PACK)]
+        d = [sb([P, S], F32, "d%d" % t) for t in range(PACK)]
         for t in range(PACK):
-            copy = nc.vector.tensor_copy if t in D_OUT_ON_VECTOR else nc.scalar.copy
-            copy(d[t][:], d_acc[t][:])
-        dw_got = sb([P, H], U32, "dw_got")
-        nc.vector.tensor_copy(dw_got[:], dw_tab[:].bitcast(U32).indirect(k1_l[:]))
-        dw = deal(nc.vector.tensor_copy, dw_got, U32, "dw")
+            nc.vector.tensor_copy(d[t][:], d_acc[t][:])
+        dw_got = pick(dw_tab, k1_l, "dw_got")
         neg_tau = sb([P, PACK], F32, "neg_tau")
         nc.vector.tensor_scalar(neg_tau[:], tau_t[:], -1.0, None, ALU.mult)
 
-        h = [sb([P, S], F32, "h%d" % t) for t in range(PACK)]
-        lows = sb([P, PACK, len(Z_CHUNKS)], F32, "lows")
-        bias = sb([P, PACK], F32, "bias")
-
-        def fetch(got, window, lst, a, b, on_vector=False, scale=1.0):
+        def fetch(got, window, offsets, on_vector=False):
             if on_vector:
-                nc.vector.tensor_copy(got, window[:].indirect(entries(lst, a, b)))
+                nc.vector.tensor_copy(got[:], window[:].indirect(offsets))
             else:
-                nc.scalar.activation(got, window[:].indirect(entries(lst, a, b)), ACT.Copy, scale=scale)
+                nc.scalar.activation(got[:], window[:].indirect(offsets), ACT.Copy)
 
         def interleave(rows, name, on_vector):
-            width = rows.shape[2]
-            mixed = sb([P, width * PACK], BF16, name)
+            mixed = sb([P, HALF * PACK], BF16, name)
             dst = mixed[:].rearrange("p (c i t) -> p c t i", i=4, t=PACK)
             src = rows[:].rearrange("p t (c i) -> p c t i", i=4)
             cut = on_vector // 4
             if on_vector > 0:
                 nc.vector.tensor_copy(dst[:, :cut], src[:, :cut])
-            if on_vector < width:
+            if on_vector < HALF:
                 nc.scalar.copy(dst[:, cut:], src[:, cut:])
             return mixed
 
-        u = sb([P, PACK, S], F32, "u", U_TAG)
+        def make_u(t, engine, after):
+            half_y1 = sb([P, S], F32, "half_y1_%d" % t)
+            nc.scalar.activation(half_y1[:], y[t][:].indirect(n1_l[:]), ACT.Copy, scale=-0.5)
+            u_t = sb([P, S], F32, "u%d" % t, after)
+            engine.tensor_tensor(u_t[:], half_y1[:], y[t][:, :S], ALU.add)
+            return u_t
 
-        def make_u(t):
-            y1 = sb([P, S], F32, "y1_%d" % t)
-            if U_ON_GPSIMD:
-                fetch(y1[:], y[t], n1_l, 0, S, scale=-0.5)
-                nc.gpsimd.tensor_tensor(u[:, t, :], y1[:], y[t][:, :S], ALU.add)
-            else:
-                fetch(y1[:], y[t], n1_l, 0, S)
-                nc.vector.scalar_tensor_tensor(u[:, t, :], y1[:], -0.5, y[t][:, :S], ALU.mult, ALU.add)
+        u = [make_u(t, nc.gpsimd, None if t else "w2s_raw") for t in range(U_TILES_ON_GPSIMD)]
+        dw = deal(nc.vector.tensor_copy, dw_got, "dw", after="half_y1_%d" % (U_TILES_ON_GPSIMD - 1))
+        u.append(make_u(PACK - 1, nc.vector, "dw_got"))
 
-        def make_z(c):
-            a, b = Z_CHUNKS[c]
-            w = b - a
-            z_rows = sb([P, PACK, w], BF16, "z_rows%d" % c)
-            lo, hi, d3 = {}, {}, {}
+        def make_z_and_multiply(half):
+            z_rows = sb([P, PACK, HALF], BF16, "z_rows%d" % half)
+            d3, lo, hi = {}, {}, {}
             for step in range(PACK + 2):
                 if step < PACK:
                     t = step
-                    d2 = sb([P, w], F32, "d2_%d_%d" % (c, t), "slot_a%d" % t if c else None)
-                    fetch(d2[:], d[t], n2_l, a, b, (c, t) in N2_ON_VECTOR)
-                    d3[t] = sb([P, w], F32, "d3_%d_%d" % (c, t), "slot_b%d" % t if c else None)
-                    fetch(d3[t][:], d[t], n3_l, a, b)
-                    lo[t] = sb([P, w], F32, "lo_%d_%d" % (c, t), None if c else "slot_a%d" % t)
-                    nc.vector.tensor_tensor(lo[t][:], u[:, t, a:b], d2[:], ALU.min)
+                    d2 = sb([P, HALF], F32, "d2_%d_%d" % (half, t), "lo_0_%d" % t if half else None)
+                    fetch(d2, d[t], entries(n2_l, half), on_vector=half == 0 and t < N2_TILES_ON_VECTOR)
+                    d3[t] = sb([P, HALF], F32, "d3_%d_%d" % (half, t), "hi_0_%d" % t if half else None)
+                    fetch(d3[t], d[t], entries(n3_l, half))
+                    lo[t] = sb([P, HALF], F32, "lo_%d_%d" % (half, t))
+                    nc.vector.tensor_tensor(lo[t][:], u[t][:, columns(half)], d2[:], ALU.min)
                 if 1 <= step <= PACK:
                     t = step - 1
-                    hi[t] = sb([P, w], F32, "hi_%d_%d" % (c, t), None if c else "slot_b%d" % t)
+                    hi[t] = sb([P, HALF], F32, "hi_%d_%d" % (half, t))
                     nc.vector.tensor_tensor(hi[t][:], lo[t][:], d3[t][:], ALU.max)
                 if step >= 2:
                     t = step - 2
-                    if c in GS_ON_SCALAR:
-                        nc.scalar.activation(z_rows[:, t, :], hi[t][:], ACT.Copy, scale=gs_t[:, t : t + 1])
-                    else:
-                        nc.vector.tensor_scalar(z_rows[:, t, :], hi[t][:], gs_t[:, t : t + 1], None, ALU.mult)
-            z_mixed = interleave(z_rows, "z_mixed%d" % c, Z_MIX_ON_VECTOR[c])
-            z_words = sb([P, w], U32, "z_words%d" % c)
-            z_plane = sb([P, w], U8, "z_plane%d" % c)
+                    nc.vector.tensor_scalar(z_rows[:, t, :], hi[t][:], gs_t[:, t : t + 1], None, ALU.mult)
+            z_mixed = interleave(z_rows, "z_mixed%d" % half, Z_MIX_ON_VECTOR[half])
+            z_words = sb([P, HALF], U32, "z_words%d" % half)
+            z_plane = sb([P, HALF], U8, "z_plane%d" % half)
             nc.vector.quantize_mx(out=z_words[:].bitcast(FP8X4), scales=z_plane[:], in_=z_mixed[:])
-            sums = []
+            sums = [bank(PACK * (1 - half) + t)[:, :HALF] for t in range(PACK)]
             for t in range(PACK):
-                acc = bank(PACK * ((c + 1) % 2) + t)
-                for n0 in range(0, w, HALF):
-                    n1_ = min(w, n0 + HALF)
-                    mx(acc[:, n0:n1_], dw, ds_plane, FP8X4, t, z_words[:, n0:n1_], z_plane[:, n0:n1_])
-                sums.append(acc[:, :w])
+                product(sums[t], dw, ds_plane, FP8X4, t, z_words, z_plane)
             return sums
 
-        def make_h(c, sums):
-            a, b = Z_CHUNKS[c]
-            for t in range(PACK):
-                if c in H_OUT_ON_SCALAR:
-                    nc.scalar.activation(h[t][:, a:b], sums[t], ACT.Copy, scale=0.0625)
-                    if c + 1 not in H_OUT_ON_SCALAR:
-                        nc.vector.tensor_reduce(lows[:, t, c : c + 1], h[t][:, :b], mybir.AxisListType.X, ALU.min)
-                else:
-                    nc.vector.tensor_scalar(
-                        h[t][:, a:b], sums[t], 0.0625, lows[:, t, c - 1 : c] if c else None, ALU.mult, ALU.min,
-                        accum_out=lows[:, t, c : c + 1],
-                    )
-                if c == len(Z_CHUNKS) - 1:
-                    nc.scalar.activation(bias[:, t : t + 1], lows[:, t, c : c + 1], ACT.Copy, scale=tau_t[:, t : t + 1])
+        h_acc = [make_z_and_multiply(half) for half in range(2)]
 
+        h = [sb([P, S], F32, "h%d" % t) for t in range(PACK)]
+        lows = sb([P, PACK, 2], F32, "lows")
+        bias = sb([P, PACK], F32, "bias")
         for t in range(PACK):
-            make_u(t)
-        sums = [make_z(c) for c in range(len(Z_CHUNKS))]
-        for c in range(len(Z_CHUNKS)):
-            make_h(c, sums[c])
+            nc.scalar.activation(h[t][:, columns(0)], h_acc[0][t], ACT.Copy, scale=0.0625)
+            nc.vector.tensor_reduce(lows[:, t, 0:1], h[t][:, columns(0)], mybir.AxisListType.X, ALU.min)
+        for t in range(PACK):
+            nc.vector.tensor_scalar(
+                h[t][:, columns(1)], h_acc[1][t], 0.0625, lows[:, t, 0:1], ALU.mult, ALU.min, accum_out=lows[:, t, 1:2]
+            )
+            nc.scalar.activation(bias[:, t : t + 1], lows[:, t, 1:2], ACT.Copy, scale=tau_t[:, t : t + 1])
 
         out_rows = out_0.rearrange("(p t) j -> p t j", t=PACK)
         out_words = out_1[0].rearrange("p c r -> p (c r)").bitcast(I32)
         o_plane = sb([P, S], U8, "o_plane")
-        for c, (a, b) in enumerate(OUT_CHUNKS):
-            w = b - a
-            o_rows = sb([P, PACK, w], F32, "o_rows%d" % c)
+        for half in range(2):
+            o_rows = sb([P, PACK, HALF], F32, "o_rows%d" % half)
             for t in range(PACK):
-                ea = sb([P, w], F32, "ea_%d_%d" % (c, t))
+                ea = sb([P, HALF], F32, "ea_%d_%d" % (half, t))
                 nc.scalar.activation(
-                    ea[:], h[t][:].indirect(entries(n4_l, a, b)), ACT.Exp,
+                    ea[:], h[t][:].indirect(entries(n4_l, half)), ACT.Exp,
                     bias=bias[:, t : t + 1], scale=neg_tau[:, t : t + 1],
                 )
-                prod = sb([P, w], F32, "prod_%d_%d" % (c, t))
-                if (c, t) in N5_ON_SCALAR + N5_EARLY:
-                    h5 = sb([P, w], F32, "h5_%d_%d" % (c, t))
-                    fetch(h5[:], h[t], n5_l, a, b, (c, t) in N5_EARLY)
+                prod = sb([P, HALF], F32, "prod_%d_%d" % (half, t))
+                if half == 1 and t == PACK - 1:
+                    h5 = sb([P, HALF], F32, "h5")
+                    fetch(h5, h[t], entries(n5_l, half))
                     nc.vector.tensor_tensor(prod[:], h5[:], ea[:], ALU.mult)
                 else:
-                    nc.vector.tensor_tensor(prod[:], h[t][:].indirect(entries(n5_l, a, b)), ea[:], ALU.mult)
-                nc.vector.scalar_tensor_tensor(o_rows[:, t, :], prod[:], -2.0, h[t][:, a:b], ALU.mult, ALU.add)
+                    nc.vector.tensor_tensor(prod[:], h[t][:].indirect(entries(n5_l, half)), ea[:], ALU.mult)
+                nc.vector.scalar_tensor_tensor(o_rows[:, t, :], prod[:], -2.0, h[t][:, columns(half)], ALU.mult, ALU.add)
                 if t % 2:
-                    nc.sync.dma_start(out_rows[:, t - 1 : t + 1, a:b], o_rows[:, t - 1 : t + 1, :])
-            o_mixed = interleave(o_rows, "o_mixed%d" % c, LAST_MIX_SPLIT if c == len(OUT_CHUNKS) - 1 else 0)
-            o_words = sb([P, w], I32, "o_words%d" % c)
-            nc.vector.quantize_mx(out=o_words[:].bitcast(FP8X4), scales=o_plane[:, a:b], in_=o_mixed[:])
-            nc.sync.dma_start(out_words[:, a:b], o_words[:])
-        for q in range(4):
+                    nc.sync.dma_start(out_rows[:, t - 1 : t + 1, columns(half)], o_rows[:, t - 1 : t + 1, :])
+            o_mixed = interleave(o_rows, "o_mixed%d" % half, OUT_MIX_ON_VECTOR[half])
+            o_words = sb([P, HALF], I32, "o_words%d" % half)
+            nc.vector.quantize_mx(out=o_words[:].bitcast(FP8X4), scales=o_plane[:, columns(half)], in_=o_mixed[:])
+            nc.sync.dma_start(out_words[:, columns(half)], o_words[:])
+        for q in range(QUADS):
             queue = nc.scalar if q % 2 else nc.sync
-            queue.dma_start(out_2[0, 4 * q : 4 * q + 4, :].bitcast(I32), o_plane[32 * q : 32 * q + 4, :].bitcast(I32))
+            queue.dma_start(
+                out_2[0, QUADS * q : QUADS * (q + 1), :].bitcast(I32), o_plane[32 * q : 32 * q + QUADS, :].bitcast(I32)
+            )

from contextlib import ExitStack

import concourse.mybir as mybir

F32 = mybir.dt.float32
BF16 = mybir.dt.bfloat16
I32 = mybir.dt.int32
U32 = mybir.dt.uint32
U16 = mybir.dt.uint16
U8 = mybir.dt.uint8
FP8X4 = mybir.dt.float8_e4m3fn_x4
FP4X4 = mybir.dt.float4_e2m1fn_x4
ALU = mybir.AluOpType
ACT = mybir.ActivationFunctionType

P = 128
PACK = 4
QUADS = 4
T, S, H, G = 1024, 512, 512, 2048
HALF = S // 2
FLOPS = 3 * 2 * 512 * 512 * 512

SPARE = 16
U_TILES_ON_GPSIMD = 3
N2_TILES_ON_VECTOR = 3
Z_MIX_ON_VECTOR = (HALF, 160)
OUT_MIX_ON_VECTOR = (0, 192)


def tile_picked_twqclampbebz_none_po_kernel(
    tc, x_words, x_scales, w1_words, w1_scales, w2_words, w2_scales, gs, d_words, d_scales, tau,
    offs, two, n1, n2, n3, k1, n4, n5, out_0, out_1, out_2,
):
    nc = tc.nc

    with ExitStack() as ctx:
        keep = ctx.enter_context(tc.tile_pool(name="keep", bufs=1))
        psum = ctx.enter_context(tc.psum_pool(name="psum", bufs=1))

        def sb(shape, dtype, name, after=None):
            return keep.tile(shape, dtype, name=name, tag=after or name, align_bytes=64)

        def bank(b):
            return psum.tile([P, S], F32, name="bank%d" % b, tag="bank%d" % b)

        def columns(half):
            return slice(HALF * half, HALF * (half + 1))

        def entries(lst, half):
            return lst[:, HALF // 16 * half : HALF // 16 * (half + 1)]

        def load_list(src, name):
            tile = sb([P, S // 16], U16, name)
            nc.sync.dma_start(tile[:], src)
            return tile

        def load_words(src, shape, dtype, name):
            tile = sb(shape, dtype, name)
            nc.sync.dma_start(tile[:].bitcast(I32), src.bitcast(I32))
            return tile

        def load_by_row_tile(src, name):
            tile = sb([P, PACK], F32, name)
            nc.sync.dma_start(tile[:], src.rearrange("(p t) o -> p (t o)", t=PACK))
            return tile

        def zeroed_plane(width, name, engine):
            tile = sb([P, width], U8, name)
            engine.memset(tile[:].bitcast(I32), 0)
            return tile

        def load_plane(tile, src, queue, quadrants):
            for q in quadrants:
                queue.dma_start(
                    tile[32 * q : 32 * q + QUADS, :].bitcast(I32), src[0, QUADS * q : QUADS * (q + 1), :].bitcast(I32)
                )

        xs_tab = zeroed_plane(T, "xs_tab", nc.gpsimd)
        w1s_raw = zeroed_plane(H, "w1s_raw", nc.gpsimd)
        w2s_raw = zeroed_plane(H, "w2s_raw", nc.vector)
        ds_tab = zeroed_plane(G, "ds_tab", nc.vector)
        ds_plane = zeroed_plane(H, "ds_plane", nc.vector)

        load_plane(xs_tab, x_scales, nc.scalar, (0, 1))
        load_plane(xs_tab, x_scales, nc.sync, (2, 3))
        offs_l = load_list(offs, "offs_l")
        load_plane(w1s_raw, w1_scales, nc.scalar, (0,))
        xw_tab = load_words(x_words[0].rearrange("p c r -> p (c r)"), [P, T], U32, "xw_tab")
        w1w_raw = load_words(w1_words[0], [P, H], U16, "w1w_raw")
        load_plane(w1s_raw, w1_scales, nc.sync, (1, 2, 3))
        w2w_raw = load_words(w2_words[0], [P, H], U16, "w2w_raw")
        two_l = load_list(two, "two_l")
        k1_l = load_list(k1, "k1_l")
        ds_rows = d_scales[0].rearrange("(g e) c -> e g c", e=2)
        for e in range(2):
            nc.sync.dma_start(ds_tab[e:P:16, :].bitcast(I32), ds_rows[e].bitcast(I32))
        load_plane(w2s_raw, w2_scales, nc.sync, range(QUADS))
        n1_l = load_list(n1, "n1_l")
        dw_tab = load_words(d_words[0].rearrange("p c r -> p (c r)"), [P, G], U32, "dw_tab")
        n2_l = load_list(n2, "n2_l")
        n3_l = load_list(n3, "n3_l")
        gs_t = load_by_row_tile(gs, "gs_t")
        tau_t = load_by_row_tile(tau, "tau_t")
        n4_l = load_list(n4, "n4_l")
        n5_l = load_list(n5, "n5_l")

        def deal(copy, raw, name, pieces=1, after=None):
            dealt = sb([P, H], raw.dtype, name, after)
            dst = dealt[:].rearrange("p (t m) -> p t m", t=PACK)
            src = raw[:].rearrange("p (m t) -> p t m", t=PACK)
            n = PACK // pieces
            for i in range(pieces):
                copy(dst[:, n * i : n * (i + 1)], src[:, n * i : n * (i + 1)])
            return dealt

        def pick(table, lst, name):
            picked = sb([P, S], table.dtype, name)
            nc.vector.tensor_copy(picked[:], table[:].indirect(lst[:]))
            return picked

        def product(acc, dealt_words, dealt_plane, fmt, t, words, plane):
            rows = slice(P * t, P * (t + 1))
            nc.tensor.matmul_mx(
                out=acc,
                lhsT=dealt_words[:, rows].bitcast(fmt),
                lhsT_scale=dealt_plane[:, rows],
                rhs=words[:].bitcast(FP8X4),
                rhs_scale=plane[:],
                start=True,
                stop=True,
            )

        w1w = deal(nc.scalar.copy, w1w_raw, "w1w")
        w1s = deal(nc.gpsimd.tensor_copy, w1s_raw, "w1s", pieces=2)
        y = [sb([P, S + SPARE], F32, "y%d" % t) for t in range(PACK)]
        for t in range(PACK):
            nc.gpsimd.memset(y[t][:, S:], 0.0)
        xq_plane = pick(xs_tab, offs_l, "xq_plane")
        xq_words = pick(xw_tab, offs_l, "xq_words")
        for t in range(PACK):
            acc = bank(PACK + t)
            product(acc[:], w1w, w1s, FP4X4, t, xq_words, xq_plane)
            nc.scalar.copy(y[t][:, :S], acc[:])

        w2w = deal(nc.scalar.copy, w2w_raw, "w2w")
        w2s = deal(nc.gpsimd.tensor_copy, w2s_raw, "w2s")
        xtwo_words = pick(xw_tab, two_l, "xtwo_words")
        xtwo_plane = pick(xs_tab, two_l, "xtwo_plane")
        d_acc = [bank(t) for t in range(PACK)]
        for t in range(PACK):
            product(d_acc[t][:], w2w, w2s, FP4X4, t, xtwo_words, xtwo_plane)

        ds_dealt = deal(nc.vector.tensor_copy, pick(ds_tab, k1_l, "ds_got"), "ds_dealt")
        for r in range(QUADS):
            first = 16 * (r // 2) + r % 2
            nc.sync.dma_start(ds_plane[r:P:32, :].bitcast(I32), ds_dealt[first:P:32, :].bitcast(I32))
        d = [sb([P, S], F32, "d%d" % t) for t in range(PACK)]
        for t in range(PACK):
            nc.vector.tensor_copy(d[t][:], d_acc[t][:])
        dw_got = pick(dw_tab, k1_l, "dw_got")
        neg_tau = sb([P, PACK], F32, "neg_tau")
        nc.vector.tensor_scalar(neg_tau[:], tau_t[:], -1.0, None, ALU.mult)

        def fetch(got, window, offsets, on_vector=False):
            if on_vector:
                nc.vector.tensor_copy(got[:], window[:].indirect(offsets))
            else:
                nc.scalar.activation(got[:], window[:].indirect(offsets), ACT.Copy)

        def interleave(rows, name, on_vector):
            mixed = sb([P, HALF * PACK], BF16, name)
            dst = mixed[:].rearrange("p (c i t) -> p c t i", i=4, t=PACK)
            src = rows[:].rearrange("p t (c i) -> p c t i", i=4)
            cut = on_vector // 4
            if on_vector > 0:
                nc.vector.tensor_copy(dst[:, :cut], src[:, :cut])
            if on_vector < HALF:
                nc.scalar.copy(dst[:, cut:], src[:, cut:])
            return mixed

        def make_u(t, engine, after):
            half_y1 = sb([P, S], F32, "half_y1_%d" % t)
            nc.scalar.activation(half_y1[:], y[t][:].indirect(n1_l[:]), ACT.Copy, scale=-0.5)
            u_t = sb([P, S], F32, "u%d" % t, after)
            engine.tensor_tensor(u_t[:], half_y1[:], y[t][:, :S], ALU.add)
            return u_t

        u = [make_u(t, nc.gpsimd, None if t else "w2s_raw") for t in range(U_TILES_ON_GPSIMD)]
        dw = deal(nc.vector.tensor_copy, dw_got, "dw", after="half_y1_%d" % (U_TILES_ON_GPSIMD - 1))
        u.append(make_u(PACK - 1, nc.vector, "dw_got"))

        def make_z_and_multiply(half):
            z_rows = sb([P, PACK, HALF], BF16, "z_rows%d" % half)
            d3, lo, hi = {}, {}, {}
            for step in range(PACK + 2):
                if step < PACK:
                    t = step
                    d2 = sb([P, HALF], F32, "d2_%d_%d" % (half, t), "lo_0_%d" % t if half else None)
                    fetch(d2, d[t], entries(n2_l, half), on_vector=half == 0 and t < N2_TILES_ON_VECTOR)
                    d3[t] = sb([P, HALF], F32, "d3_%d_%d" % (half, t), "hi_0_%d" % t if half else None)
                    fetch(d3[t], d[t], entries(n3_l, half))
                    lo[t] = sb([P, HALF], F32, "lo_%d_%d" % (half, t))
                    nc.vector.tensor_tensor(lo[t][:], u[t][:, columns(half)], d2[:], ALU.min)
                if 1 <= step <= PACK:
                    t = step - 1
                    hi[t] = sb([P, HALF], F32, "hi_%d_%d" % (half, t))
                    nc.vector.tensor_tensor(hi[t][:], lo[t][:], d3[t][:], ALU.max)
                if step >= 2:
                    t = step - 2
                    nc.vector.tensor_scalar(z_rows[:, t, :], hi[t][:], gs_t[:, t : t + 1], None, ALU.mult)
            z_mixed = interleave(z_rows, "z_mixed%d" % half, Z_MIX_ON_VECTOR[half])
            z_words = sb([P, HALF], U32, "z_words%d" % half)
            z_plane = sb([P, HALF], U8, "z_plane%d" % half)
            nc.vector.quantize_mx(out=z_words[:].bitcast(FP8X4), scales=z_plane[:], in_=z_mixed[:])
            sums = [bank(PACK * (1 - half) + t)[:, :HALF] for t in range(PACK)]
            for t in range(PACK):
                product(sums[t], dw, ds_plane, FP8X4, t, z_words, z_plane)
            return sums

        h_acc = [make_z_and_multiply(half) for half in range(2)]

        h = [sb([P, S], F32, "h%d" % t) for t in range(PACK)]
        lows = sb([P, PACK, 2], F32, "lows")
        bias = sb([P, PACK], F32, "bias")
        for t in range(PACK):
            nc.scalar.activation(h[t][:, columns(0)], h_acc[0][t], ACT.Copy, scale=0.0625)
            nc.vector.tensor_reduce(lows[:, t, 0:1], h[t][:, columns(0)], mybir.AxisListType.X, ALU.min)
        for t in range(PACK):
            nc.vector.tensor_scalar(
                h[t][:, columns(1)], h_acc[1][t], 0.0625, lows[:, t, 0:1], ALU.mult, ALU.min, accum_out=lows[:, t, 1:2]
            )
            nc.scalar.activation(bias[:, t : t + 1], lows[:, t, 1:2], ACT.Copy, scale=tau_t[:, t : t + 1])

        out_rows = out_0.rearrange("(p t) j -> p t j", t=PACK)
        out_words = out_1[0].rearrange("p c r -> p (c r)").bitcast(I32)
        o_plane = sb([P, S], U8, "o_plane")
        for half in range(2):
            o_rows = sb([P, PACK, HALF], F32, "o_rows%d" % half)
            for t in range(PACK):
                ea = sb([P, HALF], F32, "ea_%d_%d" % (half, t))
                nc.scalar.activation(
                    ea[:], h[t][:].indirect(entries(n4_l, half)), ACT.Exp,
                    bias=bias[:, t : t + 1], scale=neg_tau[:, t : t + 1],
                )
                prod = sb([P, HALF], F32, "prod_%d_%d" % (half, t))
                if half == 1 and t == PACK - 1:
                    h5 = sb([P, HALF], F32, "h5")
                    fetch(h5, h[t], entries(n5_l, half))
                    nc.vector.tensor_tensor(prod[:], h5[:], ea[:], ALU.mult)
                else:
                    nc.vector.tensor_tensor(prod[:], h[t][:].indirect(entries(n5_l, half)), ea[:], ALU.mult)
                nc.vector.scalar_tensor_tensor(o_rows[:, t, :], prod[:], -2.0, h[t][:, columns(half)], ALU.mult, ALU.add)
                if t % 2:
                    nc.sync.dma_start(out_rows[:, t - 1 : t + 1, columns(half)], o_rows[:, t - 1 : t + 1, :])
            o_mixed = interleave(o_rows, "o_mixed%d" % half, OUT_MIX_ON_VECTOR[half])
            o_words = sb([P, HALF], I32, "o_words%d" % half)
            nc.vector.quantize_mx(out=o_words[:].bitcast(FP8X4), scales=o_plane[:, columns(half)], in_=o_mixed[:])
            nc.sync.dma_start(out_words[:, columns(half)], o_words[:])
        for q in range(QUADS):
            queue = nc.scalar if q % 2 else nc.sync
            queue.dma_start(
                out_2[0, QUADS * q : QUADS * (q + 1), :].bitcast(I32), o_plane[32 * q : 32 * q + QUADS, :].bitcast(I32)
            )
